import numpy as np
import ml_dtypes


def mxq(x, axis, fmt="e4m3"):
    dtype, down = {"e4m3": (ml_dtypes.float8_e4m3fn, 7), "e5m2": (ml_dtypes.float8_e5m2, 14)}[fmt]
    v = np.moveaxis(np.asarray(x, np.float32).astype(ml_dtypes.bfloat16).astype(np.float64), axis, -1)
    blocks = v.reshape(v.shape[:-1] + (-1, 32))
    amax = np.abs(blocks).max(-1, keepdims=True)
    byte = np.maximum(np.where(amax > 0, np.frexp(amax)[1] - 1 + 127, 0) - down, 1)
    scale = np.exp2(byte - 127.0)
    codes = (blocks / scale).astype(np.float32).astype(dtype).astype(np.float64)
    return np.moveaxis((codes * scale).reshape(v.shape), -1, axis)


WIDE = False


def mx_kscale(k):
    if not WIDE:
        return np.ones(k)
    levels = np.array([10, -10, 5, -5, 0])
    if k % 512:
        return np.exp2(np.random.permutation(np.resize(levels, k // 32))).repeat(32)
    a = np.empty((k // 512, 16))
    for p in range(k // 512):
        a[p, :8] = np.random.permutation(np.resize(levels, 8))
        for g in range(8):
            far = levels[np.abs(levels - a[p, g]) >= 10]
            a[p, g + 8] = far[np.random.randint(len(far))]
    return np.exp2(a.ravel()).repeat(32)


BF16 = ml_dtypes.bfloat16


def bf(x):
    return np.asarray(x, np.float32).astype(BF16)


def f64(x):
    return np.asarray(x).astype(np.float64)


E2M1 = np.array([0.0, 0.5, 1.0, 1.5, 2.0, 3.0, 4.0, 6.0, -0.0, -0.5, -1.0, -1.5, -2.0, -3.0, -4.0, -6.0])


def pack_weight(w, fmt):
    k, n = w.shape
    w = f64(bf(w)).reshape(k // 32, 32, n)
    amax = np.abs(w).max(1)
    if fmt == "e4m3":
        byte = np.frexp(amax)[1] - 1 + 127 - 7
    else:
        mant, ex = np.frexp(amax / 6.0)
        byte = np.where(mant > 0.5, ex, ex - 1) + 127
    byte = np.clip(np.where(amax > 0, byte, 1), 1, 254)
    scaled = (w * np.exp2(127.0 - byte)[:, None, :]).reshape(k, n).astype(np.float32)
    by_word = np.ascontiguousarray(scaled.reshape(k // 512, 128, 4, n).transpose(0, 1, 3, 2))
    if fmt == "e4m3":
        words = by_word.astype(ml_dtypes.float8_e4m3fn).view(np.uint8)
    else:
        c = by_word.astype(ml_dtypes.float4_e2m1fn).view(np.uint8) & 0xF
        words = c[..., 0::2] | (c[..., 1::2] << 4)
    return np.ascontiguousarray(words), np.ascontiguousarray(byte.astype(np.uint8).reshape(k // 512, 16, n))


def unpack_weight(words, scales, fmt):
    g, p, n, _ = words.shape
    if fmt == "e4m3":
        vals = np.ascontiguousarray(words).view(ml_dtypes.float8_e4m3fn).astype(np.float64)
    else:
        nib = np.empty((g, p, n, 4), np.uint8)
        nib[..., 0::2] = words & 0xF
        nib[..., 1::2] = words >> 4
        vals = E2M1[nib]
    vals = vals * np.repeat(np.exp2(scales.astype(np.float64) - 127.0), 8, axis=1)[..., None]
    return vals.transpose(0, 1, 3, 2).reshape(g * 512, n)
def pack4(w):
    words, scales = pack_weight(w, "e2m1")
    return words.reshape(words.shape[0], 128, -1), scales


def unpack4(words, scales):
    return unpack_weight(words.reshape(words.shape[0], 128, -1, 2), scales, "e2m1")


def planes(Y):
    n, m = Y.shape
    b = f64(bf(Y)).reshape(n // 32, 32, m)
    amax = np.abs(b).max(1)
    byte = np.clip(np.where(amax > 0, np.frexp(amax)[1] - 1 + 127 - 7, 1), 1, 254)
    codes = (b * np.exp2(127.0 - byte)[:, None, :]).reshape(n, m).astype(np.float32).astype(ml_dtypes.float8_e4m3fn).view(np.uint8)
    words = codes.reshape(n // 512, 128, 4, m).transpose(0, 1, 3, 2)
    return np.ascontiguousarray(words), np.ascontiguousarray(byte.astype(np.uint8).reshape(n // 512, 16, m))


B, D, H = 512, 1024, 2048

IN_SIZE = 0.4
REC_SIZE = 0.25
LEAK = 0.35


def setup_inputs():
    s = mx_kscale(D)
    t = mx_kscale(H)
    unit = np.exp(0.8 * np.random.randn(H))
    x = np.random.randn(B, D) * s
    w_in = IN_SIZE * np.random.randn(D, H) * unit / np.sqrt(D) / s[:, None]
    h = np.random.randn(B, H) * unit * t
    rec = REC_SIZE * np.random.randn(H, H) * unit / np.sqrt(H) / t[:, None]
    leak = (LEAK + 0.05 * np.random.randn(H)) / t
    w_rec_words, w_rec_scales = pack4(rec)
    return {"x": bf(x), "w_in": bf(w_in), "h": bf(h),
            "w_rec_words": w_rec_words, "w_rec_scales": w_rec_scales,
            "leak": bf(leak)}


def reference(x, w_in, h, w_rec_words, w_rec_scales, leak):
    x, w_in, h, leak = f64(x), f64(w_in), f64(h), f64(leak)
    R = unpack4(w_rec_words, w_rec_scales)
    drive_in = mxq(x, 1, "e4m3") @ mxq(w_in, 0, "e4m3")
    drive_rec = mxq(h, 1, "e4m3") @ R
    y = leak * h + np.tanh(drive_in + drive_rec)
    Y = y.T
    words, scales = planes(Y)
    return y, words, scales

@@ -1,0 +1,265 @@
+from contextlib import ExitStack
+
+import concourse.mybir as mybir
+from concourse.masks import make_identity
+
+B, D, H = 512, 1024, 2048
+FLOPS = 2 * B * (D + H) * H
+
+F32 = mybir.dt.float32
+BF16 = mybir.dt.bfloat16
+I32 = mybir.dt.int32
+U32 = mybir.dt.uint32
+U8 = mybir.dt.uint8
+FP8X4 = mybir.dt.float8_e4m3fn_x4
+FP4X4 = mybir.dt.float4_e2m1fn_x4
+ALU = mybir.AluOpType
+ACT = mybir.ActivationFunctionType
+
+P = 128
+N = 512
+TILES = B // P
+CHUNKS = H // N
+SCALAR_COLS = (256, 128, 128, 128)
+ROUND_ON_VECTOR_FROM = 12
+
+
+def tile_leaky_recurrent_step_g4_kernel(tc, x, w_in, h, w_rec_words, w_rec_scales, leak, out_0, out_1, out_2):
+    nc = tc.nc
+    r_words = w_rec_words.bitcast(I32)
+    r_scales = w_rec_scales.bitcast(I32)
+    y_words = out_1.rearrange("g p m t -> g p (m t)").bitcast(I32)
+    y_scales = out_2.bitcast(I32)
+
+    with ExitStack() as ctx:
+        keep = ctx.enter_context(tc.tile_pool(name="keep", bufs=1))
+        turn = ctx.enter_context(tc.tile_pool(name="turn", bufs=4))
+        psum = ctx.enter_context(tc.psum_pool(name="psum", bufs=1))
+        ctx.enter_context(tc.manual_schedule(engines={mybir.EngineType.PE, mybir.EngineType.SP}))
+
+        ident = keep.tile([P, P], F32, name="ident")
+        make_identity(nc, ident[:])
+        warm = keep.tile([P, 8], F32, name="warm")
+        nc.vector.memset(warm[:], 0.0)
+        warm_out = keep.tile([P, 8], F32, name="warm_out")
+        nc.scalar.activation(out=warm_out[:], in_=warm[:], func=ACT.Tanh)
+
+        rs = []
+        for c in range(CHUNKS):
+            rs.append(keep.tile([P, 4, N], U8, name="rs%d" % c, align_bytes=64))
+            nc.vector.memset(rs[c][:].bitcast(I32), 0)
+
+        act = {}
+        rw = {}
+        w_raw = {}
+
+        def load_act(m, j):
+            act[m, j] = keep.tile([P, 1024], BF16, name="act%d%d" % (m, j), align_bytes=64)
+            rows = slice(m * P, (m + 1) * P)
+            src = x[rows, :] if j == 2 else h[rows, j * 1024 : (j + 1) * 1024]
+            nc.sync.dma_start(out=act[m, j][:], in_=src)
+
+        def load_r(c):
+            for q in range(4):
+                nc.sync.dma_start(
+                    out=rs[c][32 * q : 32 * q + 4, :, :].bitcast(I32),
+                    in_=r_scales[:, 4 * q : 4 * q + 4, c * 128 : (c + 1) * 128].rearrange("g r n -> r g n"),
+                )
+            rw[c] = keep.tile([P, 4, 2 * N], U8, name="rw%d" % c, align_bytes=64)
+            nc.sync.dma_start(
+                out=rw[c][:].bitcast(I32),
+                in_=r_words[:, :, c * 256 : (c + 1) * 256].rearrange("g p n -> p g n"),
+            )
+
+        def load_w(c, g):
+            w_raw[c, g] = keep.tile([P, 4, N], BF16, name="wraw%d%d" % (c, g), align_bytes=64)
+            nc.sync.dma_start(
+                out=w_raw[c, g][:],
+                in_=w_in[g * 512 : (g + 1) * 512, c * N : (c + 1) * N].rearrange("(p t) n -> p t n", t=4),
+            )
+
+        load_act(0, 0)
+        leak_rows = keep.tile([P, 16], BF16, name="leak_rows", align_bytes=64)
+        nc.sync.dma_start(out=leak_rows[:], in_=leak.rearrange("(q j) -> q j", j=16))
+        load_act(0, 1)
+        load_r(0)
+        for m in (1, 2):
+            load_act(m, 0)
+            load_act(m, 1)
+        load_w(0, 0)
+        load_act(3, 0)
+        load_act(3, 1)
+        load_w(0, 1)
+        for m in range(TILES):
+            load_act(m, 2)
+        for c in range(1, CHUNKS):
+            load_r(c)
+            load_w(c, 0)
+            load_w(c, 1)
+
+        turned = []
+
+        def turn_bank():
+            bank = psum.tile([P, 2, 2, P], F32, name="tp%d" % (len(turned) % 4))
+            turned.append(bank)
+            return bank
+
+        a_codes = {}
+        a_scales = {}
+
+        def stage_act(m, j):
+            words = act[m, j][:].bitcast(F32)
+            bank = turn_bank()
+            for g in range(2):
+                for u in range(2):
+                    nc.tensor.transpose(bank[:, g, u, :], words[:, 256 * g + u : 256 * (g + 1) : 2], ident[:])
+            grouped = turn.tile([P, 1024], BF16, name="grouped", align_bytes=64)
+            nc.scalar.copy(
+                out=grouped[:].bitcast(F32).rearrange("p (g r u) -> p g r u", g=2, u=2),
+                in_=bank[:].rearrange("p g u r -> p g r u"),
+            )
+            a_codes[m, j] = keep.tile([P, 256], U32, name="acodes%d%d" % (m, j), align_bytes=64)
+            a_scales[m, j] = keep.tile([P, 256], U8, name="ascales%d%d" % (m, j), align_bytes=64)
+            nc.vector.quantize_mx(out=a_codes[m, j][:].bitcast(FP8X4), scales=a_scales[m, j][:], in_=grouped[:])
+
+        leak_all = keep.tile([P, H], BF16, name="leak_all", align_bytes=64)
+
+        def spread_leak():
+            words = leak_rows[:].bitcast(F32)
+            for b in range(2):
+                bank = turn_bank()
+                flat = bank[:].rearrange("p g u q -> p (g u) q")
+                for j in range(4):
+                    col = 4 * b + j
+                    nc.tensor.transpose(flat[:, j, :], words[:, col : col + 1].to_broadcast([P, P]), ident[:])
+                nc.scalar.copy(
+                    out=leak_all[:].bitcast(F32).rearrange("p (q j) -> p q j", j=8)[:, :, 4 * b : 4 * b + 4],
+                    in_=flat.rearrange("p j q -> p q j"),
+                )
+
+        w_codes = {}
+        w_scales = {}
+
+        def stage_w(c, g):
+            wi = turn.tile([P, N, 4], BF16, name="wi", align_bytes=64, bufs=3)
+            s = SCALAR_COLS[c]
+            src = w_raw[c, g]
+            nc.scalar.copy(
+                out=wi[:, :s, :].rearrange("p (n i) t -> p n t i", i=4),
+                in_=src[:, :, :s].rearrange("p t (n i) -> p n t i", i=4),
+            )
+            nc.vector.tensor_copy(
+                out=wi[:, s:, :].rearrange("p (n i) t -> p n t i", i=4),
+                in_=src[:, :, s:].rearrange("p t (n i) -> p n t i", i=4),
+            )
+            w_codes[c, g] = keep.tile([P, N], U32, name="wcodes%d%d" % (c, g), align_bytes=64)
+            w_scales[c, g] = keep.tile([P, N], U8, name="wscales%d%d" % (c, g), align_bytes=64)
+            nc.vector.quantize_mx(
+                out=w_codes[c, g][:].bitcast(FP8X4), scales=w_scales[c, g][:], in_=wi[:].rearrange("p n t -> p (n t)")
+            )
+
+        acc = {}
+
+        def rec_passes(c, m):
+            acc[c, m] = psum.tile([P, N], F32, name="acc%d" % m)
+            for g in range(4):
+                j, cols = g // 2, slice((g % 2) * P, (g % 2 + 1) * P)
+                nc.tensor.matmul_mx(
+                    out=acc[c, m][:],
+                    lhsT=a_codes[m, j][:, cols].bitcast(FP8X4),
+                    lhsT_scale=a_scales[m, j][:, cols],
+                    rhs=rw[c][:, g, :].bitcast(FP4X4),
+                    rhs_scale=rs[c][:, g, :],
+                    start=(g == 0),
+                    stop=False,
+                )
+
+        def in_passes(c, m):
+            for g in range(2):
+                cols = slice(g * P, (g + 1) * P)
+                nc.tensor.matmul_mx(
+                    out=acc[c, m][:],
+                    lhsT=a_codes[m, 2][:, cols].bitcast(FP8X4),
+                    lhsT_scale=a_scales[m, 2][:, cols],
+                    rhs=w_codes[c, g][:].bitcast(FP8X4),
+                    rhs_scale=w_scales[c, g][:],
+                    start=False,
+                    stop=(g == 1),
+                )
+
+        y_bf = {}
+
+        def finish(c, m):
+            squashed = turn.tile([P, N], F32, name="squashed")
+            nc.scalar.activation(out=squashed[:], in_=acc[c, m][:], func=ACT.Tanh)
+            y = keep.tile([P, N], F32, name="y%d%d" % (c, m))
+            h_cols = slice((c % 2) * N, (c % 2 + 1) * N)
+            nc.vector.tensor_tensor(out=y[:], in0=act[m, c // 2][:, h_cols], in1=leak_all[:, c * N : (c + 1) * N], op=ALU.mult)
+            nc.vector.tensor_tensor(out=y[:], in0=squashed[:], in1=y[:], op=ALU.add)
+            nc.sync.dma_start(out=out_0[m * P : (m + 1) * P, c * N : (c + 1) * N], in_=y[:])
+            y_bf[c, m] = turn.tile([P, N], BF16, name="ybf", bufs=8, align_bytes=64)
+            dst = y_bf[c, m][:].rearrange("r (u p e) -> r u p e", u=2, e=2)
+            src = y[:].rearrange("r (p u e) -> r u p e", u=2, e=2)
+            if TILES * c + m >= ROUND_ON_VECTOR_FROM:
+                nc.vector.tensor_copy(out=dst, in_=src)
+            else:
+                nc.scalar.copy(out=dst, in_=src)
+
+        plane_scales = keep.tile([P, B], U8, name="plane_scales", align_bytes=64)
+        plane_codes = []
+        for c in range(CHUNKS):
+            plane_codes.append(keep.tile([P, B], U32, name="plane_codes%d" % c, align_bytes=64))
+
+        def planes(c, ms):
+            n = len(ms)
+            bank = turn_bank()
+            for i, m in enumerate(ms):
+                words = y_bf[c, m][:].bitcast(F32)
+                for u in range(2):
+                    nc.tensor.transpose(bank[:, i, u, :], words[:, u * P : (u + 1) * P], ident[:])
+            grouped = turn.tile([P, 1024], BF16, name="grouped", align_bytes=64)
+            nc.scalar.copy(
+                out=grouped[:, : n * 512].bitcast(F32).rearrange("p (i r u) -> p i r u", i=n, u=2),
+                in_=bank[:, :n, :, :].rearrange("p i u r -> p i r u"),
+            )
+            cols = slice(ms[0] * P, (ms[0] + n) * P)
+            nc.vector.quantize_mx(
+                out=plane_codes[c][:, cols].bitcast(FP8X4), scales=plane_scales[4 * c :, cols], in_=grouped[:, : n * 512]
+            )
+            nc.sync.dma_start(out=y_words[c, :, cols], in_=plane_codes[c][:, cols].bitcast(I32))
+
+        stage_act(0, 0)
+        stage_act(0, 1)
+        spread_leak()
+        rec_passes(0, 0)
+        for m in (1, 2):
+            stage_act(m, 0)
+            stage_act(m, 1)
+        rec_passes(0, 1)
+        stage_act(3, 0)
+        stage_act(3, 1)
+        rec_passes(0, 2)
+        stage_act(0, 2)
+        stage_act(1, 2)
+        rec_passes(0, 3)
+        stage_act(2, 2)
+        stage_act(3, 2)
+        for c in range(CHUNKS):
+            stage_w(c, 0)
+            stage_w(c, 1)
+            for m in range(TILES):
+                if c > 0:
+                    rec_passes(c, m)
+                in_passes(c, m)
+                if c > 0 and m == 2:
+                    planes(c - 1, (0, 1))
+                    planes(c - 1, (2, 3))
+                finish(c, m)
+        planes(3, (0, 1))
+        planes(3, (2,))
+        planes(3, (3,))
+        for q in range(4):
+            eng = nc.sync if q < 2 else nc.scalar
+            eng.dma_start(
+                out=y_scales[:, 4 * q : 4 * q + 4, :], in_=plane_scales[32 * q : 32 * q + 16, :].bitcast(I32)
+            )

@@ -20,7 +20,7 @@ P = 128
 N = 512
 TILES = B // P
 CHUNKS = H // N
-SCALAR_COLS = (256, 128, 128, 128)
+SCALAR_COLS = (256, 256, 128, 128)
 ROUND_ON_VECTOR_FROM = 12
 
 
@@ -35,14 +35,10 @@ def tile_leaky_recurrent_step_g4_kernel(tc, x, w_in, h, w_rec_words, w_rec_scale
         keep = ctx.enter_context(tc.tile_pool(name="keep", bufs=1))
         turn = ctx.enter_context(tc.tile_pool(name="turn", bufs=4))
         psum = ctx.enter_context(tc.psum_pool(name="psum", bufs=1))
-        ctx.enter_context(tc.manual_schedule(engines={mybir.EngineType.PE, mybir.EngineType.SP}))
+        ctx.enter_context(tc.manual_schedule())
 
         ident = keep.tile([P, P], F32, name="ident")
         make_identity(nc, ident[:])
-        warm = keep.tile([P, 8], F32, name="warm")
-        nc.vector.memset(warm[:], 0.0)
-        warm_out = keep.tile([P, 8], F32, name="warm_out")
-        nc.scalar.activation(out=warm_out[:], in_=warm[:], func=ACT.Tanh)
 
         rs = []
         for c in range(CHUNKS):
@@ -53,23 +49,33 @@ def tile_leaky_recurrent_step_g4_kernel(tc, x, w_in, h, w_rec_words, w_rec_scale
         rw = {}
         w_raw = {}
 
-        def load_act(m, j):
-            act[m, j] = keep.tile([P, 1024], BF16, name="act%d%d" % (m, j), align_bytes=64)
-            rows = slice(m * P, (m + 1) * P)
-            src = x[rows, :] if j == 2 else h[rows, j * 1024 : (j + 1) * 1024]
-            nc.sync.dma_start(out=act[m, j][:], in_=src)
+        def load_h(m, halves):
+            tile = keep.tile([P, len(halves) * 1024], BF16, name="h%d%d" % (m, halves[0]), align_bytes=64)
+            nc.sync.dma_start(out=tile[:], in_=h[m * P : (m + 1) * P, halves[0] * 1024 : (halves[-1] + 1) * 1024])
+            for i, j in enumerate(halves):
+                act[m, j] = tile[:, i * 1024 : (i + 1) * 1024]
 
-        def load_r(c):
+        def load_x(m):
+            tile = keep.tile([P, 2, D], BF16, name="x%d" % m, align_bytes=64)
+            nc.sync.dma_start(out=tile[:], in_=x[m * P : (m + 2) * P, :].rearrange("(i r) k -> r i k", i=2))
+            for i in range(2):
+                act[m + i, 2] = tile[:, i, :]
+
+        def load_r_scales(c):
             for q in range(4):
                 nc.sync.dma_start(
                     out=rs[c][32 * q : 32 * q + 4, :, :].bitcast(I32),
                     in_=r_scales[:, 4 * q : 4 * q + 4, c * 128 : (c + 1) * 128].rearrange("g r n -> r g n"),
                 )
-            rw[c] = keep.tile([P, 4, 2 * N], U8, name="rw%d" % c, align_bytes=64)
+
+        def load_r_words(c, g0, g1):
+            tile = keep.tile([P, g1 - g0, 2 * N], U8, name="rw%d%d" % (c, g0), align_bytes=64)
             nc.sync.dma_start(
-                out=rw[c][:].bitcast(I32),
-                in_=r_words[:, :, c * 256 : (c + 1) * 256].rearrange("g p n -> p g n"),
+                out=tile[:].bitcast(I32),
+                in_=r_words[g0:g1, :, c * 256 : (c + 1) * 256].rearrange("g p n -> p g n"),
             )
+            for g in range(g0, g1):
+                rw[c, g] = tile[:, g - g0, :]
 
         def load_w(c, g):
             w_raw[c, g] = keep.tile([P, 4, N], BF16, name="wraw%d%d" % (c, g), align_bytes=64)
@@ -78,22 +84,23 @@ def tile_leaky_recurrent_step_g4_kernel(tc, x, w_in, h, w_rec_words, w_rec_scale
                 in_=w_in[g * 512 : (g + 1) * 512, c * N : (c + 1) * N].rearrange("(p t) n -> p t n", t=4),
             )
 
-        load_act(0, 0)
         leak_rows = keep.tile([P, 16], BF16, name="leak_rows", align_bytes=64)
         nc.sync.dma_start(out=leak_rows[:], in_=leak.rearrange("(q j) -> q j", j=16))
-        load_act(0, 1)
-        load_r(0)
-        for m in (1, 2):
-            load_act(m, 0)
-            load_act(m, 1)
+        load_h(0, (0,))
+        load_r_scales(0)
+        load_r_words(0, 0, 2)
+        load_h(0, (1,))
+        load_r_words(0, 2, 4)
+        load_h(1, (0, 1))
+        load_h(2, (0, 1))
         load_w(0, 0)
-        load_act(3, 0)
-        load_act(3, 1)
+        load_x(0)
         load_w(0, 1)
-        for m in range(TILES):
-            load_act(m, 2)
+        load_h(3, (0, 1))
+        load_x(2)
         for c in range(1, CHUNKS):
-            load_r(c)
+            load_r_scales(c)
+            load_r_words(c, 0, 4)
             load_w(c, 0)
             load_w(c, 1)
 
@@ -107,41 +114,66 @@ def tile_leaky_recurrent_step_g4_kernel(tc, x, w_in, h, w_rec_words, w_rec_scale
         a_codes = {}
         a_scales = {}
 
-        def stage_act(m, j):
-            words = act[m, j][:].bitcast(F32)
-            bank = turn_bank()
+        a_bank = {}
+        a_grouped = {}
+
+        def turn_act(m, j):
+            words = act[m, j].bitcast(F32)
+            a_bank[m, j] = turn_bank()
             for g in range(2):
                 for u in range(2):
-                    nc.tensor.transpose(bank[:, g, u, :], words[:, 256 * g + u : 256 * (g + 1) : 2], ident[:])
-            grouped = turn.tile([P, 1024], BF16, name="grouped", align_bytes=64)
-            nc.scalar.copy(
-                out=grouped[:].bitcast(F32).rearrange("p (g r u) -> p g r u", g=2, u=2),
-                in_=bank[:].rearrange("p g u r -> p g r u"),
+                    nc.tensor.transpose(a_bank[m, j][:, g, u, :], words[:, 256 * g + u : 256 * (g + 1) : 2], ident[:])
+
+        def unload_act(m, j, copy):
+            a_grouped[m, j] = turn.tile([P, 1024], BF16, name="grouped", align_bytes=64)
+            copy(
+                out=a_grouped[m, j][:].bitcast(F32).rearrange("p (g r u) -> p g r u", g=2, u=2),
+                in_=a_bank[m, j][:].rearrange("p g u r -> p g r u"),
             )
+
+        def quant_act(m, j):
             a_codes[m, j] = keep.tile([P, 256], U32, name="acodes%d%d" % (m, j), align_bytes=64)
             a_scales[m, j] = keep.tile([P, 256], U8, name="ascales%d%d" % (m, j), align_bytes=64)
-            nc.vector.quantize_mx(out=a_codes[m, j][:].bitcast(FP8X4), scales=a_scales[m, j][:], in_=grouped[:])
+            nc.vector.quantize_mx(out=a_codes[m, j][:].bitcast(FP8X4), scales=a_scales[m, j][:], in_=a_grouped[m, j][:])
+
+        def turn_pair(a, b):
+            turn_act(*a)
+            turn_act(*b)
+            unload_act(*a, nc.scalar.copy)
+            unload_act(*b, nc.scalar.copy)
+
+        def quant_pair(a, b):
+            quant_act(*a)
+            quant_act(*b)
 
         leak_all = keep.tile([P, H], BF16, name="leak_all", align_bytes=64)
 
-        def spread_leak():
+        def spread_leak(b):
             words = leak_rows[:].bitcast(F32)
-            for b in range(2):
-                bank = turn_bank()
-                flat = bank[:].rearrange("p g u q -> p (g u) q")
-                for j in range(4):
-                    col = 4 * b + j
-                    nc.tensor.transpose(flat[:, j, :], words[:, col : col + 1].to_broadcast([P, P]), ident[:])
+            bank = turn_bank()
+            flat = bank[:].rearrange("p g u q -> p (g u) q")
+            for j in range(4):
+                col = 4 * b + j
+                nc.tensor.transpose(flat[:, j, :], words[:, col : col + 1].to_broadcast([P, P]), ident[:])
+            if b == 0:
+                nc.scalar.activation(
+                    out=leak_all[:].rearrange("p (q j e) -> p q j e", j=8, e=2)[:, :, :4, :],
+                    in_=bank[:].rearrange("p g u q -> p (g u q)").bitcast(BF16).rearrange("p (j q e) -> p q j e", j=4, e=2),
+                    func=ACT.Copy,
+                )
+            else:
                 nc.scalar.copy(
-                    out=leak_all[:].bitcast(F32).rearrange("p (q j) -> p q j", j=8)[:, :, 4 * b : 4 * b + 4],
+                    out=leak_all[:].bitcast(F32).rearrange("p (q j) -> p q j", j=8)[:, :, 4:],
                     in_=flat.rearrange("p j q -> p q j"),
                 )
 
         w_codes = {}
         w_scales = {}
+        w_grouped = {}
 
-        def stage_w(c, g):
+        def group_w(c, g):
             wi = turn.tile([P, N, 4], BF16, name="wi", align_bytes=64, bufs=3)
+            w_grouped[c, g] = wi
             s = SCALAR_COLS[c]
             src = w_raw[c, g]
             nc.scalar.copy(
@@ -152,23 +184,28 @@ def tile_leaky_recurrent_step_g4_kernel(tc, x, w_in, h, w_rec_words, w_rec_scale
                 out=wi[:, s:, :].rearrange("p (n i) t -> p n t i", i=4),
                 in_=src[:, :, s:].rearrange("p t (n i) -> p n t i", i=4),
             )
+
+        def quant_w(c, g):
             w_codes[c, g] = keep.tile([P, N], U32, name="wcodes%d%d" % (c, g), align_bytes=64)
             w_scales[c, g] = keep.tile([P, N], U8, name="wscales%d%d" % (c, g), align_bytes=64)
             nc.vector.quantize_mx(
-                out=w_codes[c, g][:].bitcast(FP8X4), scales=w_scales[c, g][:], in_=wi[:].rearrange("p n t -> p (n t)")
+                out=w_codes[c, g][:].bitcast(FP8X4),
+                scales=w_scales[c, g][:],
+                in_=w_grouped[c, g][:].rearrange("p n t -> p (n t)"),
             )
 
         acc = {}
 
-        def rec_passes(c, m):
-            acc[c, m] = psum.tile([P, N], F32, name="acc%d" % m)
-            for g in range(4):
+        def rec_passes(c, m, g0=0, g1=4):
+            if g0 == 0:
+                acc[c, m] = psum.tile([P, N], F32, name="acc%d" % m)
+            for g in range(g0, g1):
                 j, cols = g // 2, slice((g % 2) * P, (g % 2 + 1) * P)
                 nc.tensor.matmul_mx(
                     out=acc[c, m][:],
                     lhsT=a_codes[m, j][:, cols].bitcast(FP8X4),
                     lhsT_scale=a_scales[m, j][:, cols],
-                    rhs=rw[c][:, g, :].bitcast(FP4X4),
+                    rhs=rw[c, g].bitcast(FP4X4),
                     rhs_scale=rs[c][:, g, :],
                     start=(g == 0),
                     stop=False,
@@ -187,77 +224,154 @@ def tile_leaky_recurrent_step_g4_kernel(tc, x, w_in, h, w_rec_words, w_rec_scale
                     stop=(g == 1),
                 )
 
+        y = {}
         y_bf = {}
+        squashed = {}
 
-        def finish(c, m):
-            squashed = turn.tile([P, N], F32, name="squashed")
-            nc.scalar.activation(out=squashed[:], in_=acc[c, m][:], func=ACT.Tanh)
-            y = keep.tile([P, N], F32, name="y%d%d" % (c, m))
+        def decay(k):
+            c, m = divmod(k, TILES)
+            y[k] = keep.tile([P, N], F32, name="y%d" % k)
             h_cols = slice((c % 2) * N, (c % 2 + 1) * N)
-            nc.vector.tensor_tensor(out=y[:], in0=act[m, c // 2][:, h_cols], in1=leak_all[:, c * N : (c + 1) * N], op=ALU.mult)
-            nc.vector.tensor_tensor(out=y[:], in0=squashed[:], in1=y[:], op=ALU.add)
-            nc.sync.dma_start(out=out_0[m * P : (m + 1) * P, c * N : (c + 1) * N], in_=y[:])
-            y_bf[c, m] = turn.tile([P, N], BF16, name="ybf", bufs=8, align_bytes=64)
-            dst = y_bf[c, m][:].rearrange("r (u p e) -> r u p e", u=2, e=2)
-            src = y[:].rearrange("r (p u e) -> r u p e", u=2, e=2)
-            if TILES * c + m >= ROUND_ON_VECTOR_FROM:
-                nc.vector.tensor_copy(out=dst, in_=src)
-            else:
-                nc.scalar.copy(out=dst, in_=src)
+            nc.vector.tensor_tensor(out=y[k][:], in0=act[m, c // 2][:, h_cols], in1=leak_all[:, c * N : (c + 1) * N], op=ALU.mult)
+
+        def squash(k):
+            squashed[k] = turn.tile([P, N], F32, name="squashed")
+            nc.scalar.activation(out=squashed[k][:], in_=acc[divmod(k, TILES)][:], func=ACT.Tanh)
+
+        def add_up(k):
+            c, m = divmod(k, TILES)
+            nc.vector.tensor_tensor(out=y[k][:], in0=squashed[k][:], in1=y[k][:], op=ALU.add)
+            nc.sync.dma_start(out=out_0[m * P : (m + 1) * P, c * N : (c + 1) * N], in_=y[k][:])
+
+        def round_y(k, copy):
+            y_bf[k] = turn.tile([P, N], BF16, name="ybf", bufs=8, align_bytes=64)
+            copy(
+                out=y_bf[k][:].rearrange("r (u p e) -> r u p e", u=2, e=2),
+                in_=y[k][:].rearrange("r (p u e) -> r u p e", u=2, e=2),
+            )
 
         plane_scales = keep.tile([P, B], U8, name="plane_scales", align_bytes=64)
         plane_codes = []
         for c in range(CHUNKS):
             plane_codes.append(keep.tile([P, B], U32, name="plane_codes%d" % c, align_bytes=64))
 
-        def planes(c, ms):
+        y_grouped = {}
+
+        def turn_y(c, ms):
             n = len(ms)
             bank = turn_bank()
             for i, m in enumerate(ms):
-                words = y_bf[c, m][:].bitcast(F32)
+                words = y_bf[TILES * c + m][:].bitcast(F32)
                 for u in range(2):
                     nc.tensor.transpose(bank[:, i, u, :], words[:, u * P : (u + 1) * P], ident[:])
-            grouped = turn.tile([P, 1024], BF16, name="grouped", align_bytes=64)
+            y_grouped[c, ms] = turn.tile([P, 1024], BF16, name="grouped", align_bytes=64)
             nc.scalar.copy(
-                out=grouped[:, : n * 512].bitcast(F32).rearrange("p (i r u) -> p i r u", i=n, u=2),
+                out=y_grouped[c, ms][:, : n * 512].bitcast(F32).rearrange("p (i r u) -> p i r u", i=n, u=2),
                 in_=bank[:, :n, :, :].rearrange("p i u r -> p i r u"),
             )
+
+        def quant_y(c, ms):
+            n = len(ms)
             cols = slice(ms[0] * P, (ms[0] + n) * P)
             nc.vector.quantize_mx(
-                out=plane_codes[c][:, cols].bitcast(FP8X4), scales=plane_scales[4 * c :, cols], in_=grouped[:, : n * 512]
+                out=plane_codes[c][:, cols].bitcast(FP8X4),
+                scales=plane_scales[4 * c :, cols],
+                in_=y_grouped[c, ms][:, : n * 512],
             )
             nc.sync.dma_start(out=y_words[c, :, cols], in_=plane_codes[c][:, cols].bitcast(I32))
 
-        stage_act(0, 0)
-        stage_act(0, 1)
-        spread_leak()
-        rec_passes(0, 0)
-        for m in (1, 2):
-            stage_act(m, 0)
-            stage_act(m, 1)
+        spread_leak(0)
+        turn_act(0, 0)
+        unload_act(0, 0, nc.vector.tensor_copy)
+        quant_act(0, 0)
+        spread_leak(1)
+        turn_act(0, 1)
+        unload_act(0, 1, nc.scalar.copy)
+        decay(0)
+        decay(4)
+        quant_act(0, 1)
+        rec_passes(0, 0, 0, 2)
+        turn_pair((1, 0), (1, 1))
+        decay(1)
+        decay(5)
+        decay(8)
+        rec_passes(0, 0, 2, 4)
+        quant_pair((1, 0), (1, 1))
+        group_w(0, 0)
+        turn_pair((2, 0), (2, 1))
+        quant_w(0, 0)
+        quant_pair((2, 0), (2, 1))
+        group_w(0, 1)
         rec_passes(0, 1)
-        stage_act(3, 0)
-        stage_act(3, 1)
+        turn_pair((0, 2), (1, 2))
+        quant_w(0, 1)
+        quant_pair((0, 2), (1, 2))
+        decay(2)
+        decay(3)
         rec_passes(0, 2)
-        stage_act(0, 2)
-        stage_act(1, 2)
+        turn_pair((3, 0), (3, 1))
+        quant_pair((3, 0), (3, 1))
+        in_passes(0, 0)
+        in_passes(0, 1)
+        group_w(1, 0)
+        turn_pair((2, 2), (3, 2))
+        quant_w(1, 0)
+        quant_pair((2, 2), (3, 2))
+        group_w(1, 1)
+        squash(0)
+        squash(1)
+        quant_w(1, 1)
+        add_up(0)
         rec_passes(0, 3)
-        stage_act(2, 2)
-        stage_act(3, 2)
-        for c in range(CHUNKS):
-            stage_w(c, 0)
-            stage_w(c, 1)
-            for m in range(TILES):
-                if c > 0:
-                    rec_passes(c, m)
-                in_passes(c, m)
-                if c > 0 and m == 2:
-                    planes(c - 1, (0, 1))
-                    planes(c - 1, (2, 3))
-                finish(c, m)
-        planes(3, (0, 1))
-        planes(3, (2,))
-        planes(3, (3,))
+        add_up(1)
+        round_y(0, nc.scalar.copy)
+
+        decay_at = {2: 6, 3: 7, 6: 9, 7: 10, 9: 11, 10: 12, 11: 13, 12: 14, 13: 15}
+        group_at = {3: (2, 0), 5: (2, 1), 7: (3, 0), 9: (3, 1)}
+        planes_at = {7: 0, 11: 1}
+        for k in range(2, 15):
+            c, m = divmod(k, TILES)
+            if c > 0:
+                rec_passes(c, m)
+            in_passes(c, m)
+            if k >= 3:
+                squash(k - 1)
+                if k - 2 < ROUND_ON_VECTOR_FROM:
+                    round_y(k - 2, nc.scalar.copy)
+            if k in planes_at:
+                turn_y(planes_at[k], (0, 1))
+                turn_y(planes_at[k], (2, 3))
+            if k in decay_at:
+                decay(decay_at[k])
+            if k >= 3:
+                add_up(k - 1)
+            if k - 1 in group_at:
+                quant_w(*group_at[k - 1])
+            if k in group_at:
+                group_w(*group_at[k])
+            if k - 1 >= ROUND_ON_VECTOR_FROM:
+                round_y(k - 1, nc.vector.tensor_copy)
+            if k in planes_at:
+                quant_y(planes_at[k], (0, 1))
+                quant_y(planes_at[k], (2, 3))
+        squash(14)
+        turn_y(2, (0, 1))
+        turn_y(2, (2, 3))
+        rec_passes(3, 3)
+        in_passes(3, 3)
+        add_up(14)
+        quant_y(2, (0, 1))
+        round_y(14, nc.vector.tensor_copy)
+        quant_y(2, (2, 3))
+        squash(15)
+        turn_y(3, (0, 1))
+        turn_y(3, (2,))
+        add_up(15)
+        quant_y(3, (0, 1))
+        round_y(15, nc.vector.tensor_copy)
+        quant_y(3, (2,))
+        turn_y(3, (3,))
+        quant_y(3, (3,))
         for q in range(4):
             eng = nc.sync if q < 2 else nc.scalar
             eng.dma_start(

@@ -46,6 +46,8 @@ def tile_leaky_recurrent_step_g4_kernel(tc, x, w_in, h, w_rec_words, w_rec_scale
             nc.vector.memset(rs[c][:].bitcast(I32), 0)
 
         act = {}
+        x_raw = {}
+        x_sorted = {}
         rw = {}
         w_raw = {}
 
@@ -58,8 +60,7 @@ def tile_leaky_recurrent_step_g4_kernel(tc, x, w_in, h, w_rec_words, w_rec_scale
         def load_x(m):
             tile = keep.tile([P, 2, D], BF16, name="x%d" % m, align_bytes=64)
             nc.sync.dma_start(out=tile[:], in_=x[m * P : (m + 2) * P, :].rearrange("(i r) k -> r i k", i=2))
-            for i in range(2):
-                act[m + i, 2] = tile[:, i, :]
+            x_raw[m] = tile
 
         def load_r_scales(c):
             for q in range(4):
@@ -87,9 +88,9 @@ def tile_leaky_recurrent_step_g4_kernel(tc, x, w_in, h, w_rec_words, w_rec_scale
         leak_rows = keep.tile([P, 16], BF16, name="leak_rows", align_bytes=64)
         nc.sync.dma_start(out=leak_rows[:], in_=leak.rearrange("(q j) -> q j", j=16))
         load_h(0, (0,))
+        load_h(0, (1,))
         load_r_scales(0)
         load_r_words(0, 0, 2)
-        load_h(0, (1,))
         load_r_words(0, 2, 4)
         load_h(1, (0, 1))
         load_h(2, (0, 1))
@@ -99,10 +100,10 @@ def tile_leaky_recurrent_step_g4_kernel(tc, x, w_in, h, w_rec_words, w_rec_scale
         load_h(3, (0, 1))
         load_x(2)
         for c in range(1, CHUNKS):
-            load_r_scales(c)
-            load_r_words(c, 0, 4)
             load_w(c, 0)
             load_w(c, 1)
+            load_r_scales(c)
+            load_r_words(c, 0, 4)
 
         turned = []
 
@@ -117,15 +118,25 @@ def tile_leaky_recurrent_step_g4_kernel(tc, x, w_in, h, w_rec_words, w_rec_scale
         a_bank = {}
         a_grouped = {}
 
+        def sort_x(m):
+            tile = keep.tile([P, 4, 2, P], F32, name="xsorted%d" % m, align_bytes=64)
+            words = x_raw[m][:].rearrange("r i k -> r (i k)").bitcast(F32)
+            nc.vector.tensor_copy(out=tile[:], in_=words.rearrange("r (a p u) -> r a u p", a=4, u=2))
+            for i in range(2):
+                x_sorted[m + i] = tile[:, 2 * i : 2 * i + 2, :, :]
+
         def turn_act(m, j):
-            words = act[m, j].bitcast(F32)
             a_bank[m, j] = turn_bank()
             for g in range(2):
                 for u in range(2):
-                    nc.tensor.transpose(a_bank[m, j][:, g, u, :], words[:, 256 * g + u : 256 * (g + 1) : 2], ident[:])
+                    if j == 2:
+                        src = x_sorted[m][:, g, u, :]
+                    else:
+                        src = act[m, j].bitcast(F32)[:, 256 * g + u : 256 * (g + 1) : 2]
+                    nc.tensor.transpose(a_bank[m, j][:, g, u, :], src, ident[:])
 
-        def unload_act(m, j, copy):
-            a_grouped[m, j] = turn.tile([P, 1024], BF16, name="grouped", align_bytes=64)
+        def unload_act(m, j, copy=nc.scalar.copy):
+            a_grouped[m, j] = turn.tile([P, 1024], BF16, name="grouped", align_bytes=64, bufs=6)
             copy(
                 out=a_grouped[m, j][:].bitcast(F32).rearrange("p (g r u) -> p g r u", g=2, u=2),
                 in_=a_bank[m, j][:].rearrange("p g u r -> p g r u"),
@@ -135,16 +146,6 @@ def tile_leaky_recurrent_step_g4_kernel(tc, x, w_in, h, w_rec_words, w_rec_scale
             a_codes[m, j] = keep.tile([P, 256], U32, name="acodes%d%d" % (m, j), align_bytes=64)
             a_scales[m, j] = keep.tile([P, 256], U8, name="ascales%d%d" % (m, j), align_bytes=64)
             nc.vector.quantize_mx(out=a_codes[m, j][:].bitcast(FP8X4), scales=a_scales[m, j][:], in_=a_grouped[m, j][:])
-
-        def turn_pair(a, b):
-            turn_act(*a)
-            turn_act(*b)
-            unload_act(*a, nc.scalar.copy)
-            unload_act(*b, nc.scalar.copy)
-
-        def quant_pair(a, b):
-            quant_act(*a)
-            quant_act(*b)
 
         leak_all = keep.tile([P, H], BF16, name="leak_all", align_bytes=64)
 
@@ -171,19 +172,19 @@ def tile_leaky_recurrent_step_g4_kernel(tc, x, w_in, h, w_rec_words, w_rec_scale
         w_scales = {}
         w_grouped = {}
 
-        def group_w(c, g):
-            wi = turn.tile([P, N, 4], BF16, name="wi", align_bytes=64, bufs=3)
-            w_grouped[c, g] = wi
-            s = SCALAR_COLS[c]
-            src = w_raw[c, g]
-            nc.scalar.copy(
-                out=wi[:, :s, :].rearrange("p (n i) t -> p n t i", i=4),
-                in_=src[:, :, :s].rearrange("p t (n i) -> p n t i", i=4),
+        def group_w(c, g, copy, cols):
+            if (c, g) not in w_grouped:
+                w_grouped[c, g] = turn.tile([P, N, 4], BF16, name="wi", align_bytes=64, bufs=3)
+            copy(
+                out=w_grouped[c, g][:, cols, :].rearrange("p (n i) t -> p n t i", i=4),
+                in_=w_raw[c, g][:, :, cols].rearrange("p t (n i) -> p n t i", i=4),
             )
-            nc.vector.tensor_copy(
-                out=wi[:, s:, :].rearrange("p (n i) t -> p n t i", i=4),
-                in_=src[:, :, s:].rearrange("p t (n i) -> p n t i", i=4),
-            )
+
+        def group_w_scalar(c, g):
+            group_w(c, g, nc.scalar.copy, slice(0, SCALAR_COLS[c]))
+
+        def group_w_vector(c, g):
+            group_w(c, g, nc.vector.tensor_copy, slice(SCALAR_COLS[c], N))
 
         def quant_w(c, g):
             w_codes[c, g] = keep.tile([P, N], U32, name="wcodes%d%d" % (c, g), align_bytes=64)
@@ -196,33 +197,39 @@ def tile_leaky_recurrent_step_g4_kernel(tc, x, w_in, h, w_rec_words, w_rec_scale
 
         acc = {}
 
+        def rec_pass(c, m, g, out, n0, n1):
+            j, cols = g // 2, slice((g % 2) * P, (g % 2 + 1) * P)
+            nc.tensor.matmul_mx(
+                out=out,
+                lhsT=a_codes[m, j][:, cols].bitcast(FP8X4),
+                lhsT_scale=a_scales[m, j][:, cols],
+                rhs=rw[c, g][:, 2 * n0 : 2 * n1].bitcast(FP4X4),
+                rhs_scale=rs[c][:, g, n0:n1],
+                start=(g == 0),
+                stop=False,
+            )
+
+        def in_pass(c, m, g, out, n0, n1):
+            cols = slice(g * P, (g + 1) * P)
+            nc.tensor.matmul_mx(
+                out=out,
+                lhsT=a_codes[m, 2][:, cols].bitcast(FP8X4),
+                lhsT_scale=a_scales[m, 2][:, cols],
+                rhs=w_codes[c, g][:, n0:n1].bitcast(FP8X4),
+                rhs_scale=w_scales[c, g][:, n0:n1],
+                start=False,
+                stop=(g == 1),
+            )
+
         def rec_passes(c, m, g0=0, g1=4):
             if g0 == 0:
                 acc[c, m] = psum.tile([P, N], F32, name="acc%d" % m)
             for g in range(g0, g1):
-                j, cols = g // 2, slice((g % 2) * P, (g % 2 + 1) * P)
-                nc.tensor.matmul_mx(
-                    out=acc[c, m][:],
-                    lhsT=a_codes[m, j][:, cols].bitcast(FP8X4),
-                    lhsT_scale=a_scales[m, j][:, cols],
-                    rhs=rw[c, g].bitcast(FP4X4),
-                    rhs_scale=rs[c][:, g, :],
-                    start=(g == 0),
-                    stop=False,
-                )
+                rec_pass(c, m, g, acc[c, m][:], 0, N)
 
         def in_passes(c, m):
             for g in range(2):
-                cols = slice(g * P, (g + 1) * P)
-                nc.tensor.matmul_mx(
-                    out=acc[c, m][:],
-                    lhsT=a_codes[m, 2][:, cols].bitcast(FP8X4),
-                    lhsT_scale=a_scales[m, 2][:, cols],
-                    rhs=w_codes[c, g][:].bitcast(FP8X4),
-                    rhs_scale=w_scales[c, g][:],
-                    start=False,
-                    stop=(g == 1),
-                )
+                in_pass(c, m, g, acc[c, m][:], 0, N)
 
         y = {}
         y_bf = {}
@@ -264,7 +271,7 @@ def tile_leaky_recurrent_step_g4_kernel(tc, x, w_in, h, w_rec_words, w_rec_scale
                 words = y_bf[TILES * c + m][:].bitcast(F32)
                 for u in range(2):
                     nc.tensor.transpose(bank[:, i, u, :], words[:, u * P : (u + 1) * P], ident[:])
-            y_grouped[c, ms] = turn.tile([P, 1024], BF16, name="grouped", align_bytes=64)
+            y_grouped[c, ms] = turn.tile([P, 1024], BF16, name="grouped", align_bytes=64, bufs=6)
             nc.scalar.copy(
                 out=y_grouped[c, ms][:, : n * 512].bitcast(F32).rearrange("p (i r u) -> p i r u", i=n, u=2),
                 in_=bank[:, :n, :, :].rearrange("p i u r -> p i r u"),
@@ -284,45 +291,71 @@ def tile_leaky_recurrent_step_g4_kernel(tc, x, w_in, h, w_rec_words, w_rec_scale
         turn_act(0, 0)
         unload_act(0, 0, nc.vector.tensor_copy)
         quant_act(0, 0)
-        spread_leak(1)
         turn_act(0, 1)
-        unload_act(0, 1, nc.scalar.copy)
-        decay(0)
-        decay(4)
+        unload_act(0, 1)
+        spread_leak(1)
         quant_act(0, 1)
         rec_passes(0, 0, 0, 2)
-        turn_pair((1, 0), (1, 1))
+        decay(0)
+        decay(4)
+        turn_act(1, 0)
+        unload_act(1, 0)
         decay(1)
         decay(5)
-        decay(8)
+        group_w_vector(0, 0)
+        group_w_scalar(0, 0)
+        turn_act(1, 1)
+        quant_act(1, 0)
+        sort_x(0)
+        unload_act(1, 1)
         rec_passes(0, 0, 2, 4)
-        quant_pair((1, 0), (1, 1))
-        group_w(0, 0)
-        turn_pair((2, 0), (2, 1))
-        quant_w(0, 0)
-        quant_pair((2, 0), (2, 1))
-        group_w(0, 1)
-        rec_passes(0, 1)
-        turn_pair((0, 2), (1, 2))
-        quant_w(0, 1)
-        quant_pair((0, 2), (1, 2))
         decay(2)
+        quant_w(0, 0)
+        turn_act(2, 0)
+        turn_act(2, 1)
+        turn_act(0, 2)
+        unload_act(2, 0)
+        unload_act(2, 1)
+        unload_act(0, 2)
+        quant_act(1, 1)
+        quant_act(2, 0)
+        group_w_vector(0, 1)
+        quant_act(2, 1)
+        quant_act(0, 2)
+        rec_passes(0, 1)
+        group_w_scalar(0, 1)
+        sort_x(2)
+        turn_act(1, 2)
+        turn_act(3, 0)
+        turn_act(3, 1)
+        unload_act(1, 2)
+        unload_act(3, 0)
+        unload_act(3, 1)
+        quant_w(0, 1)
+        quant_act(1, 2)
         decay(3)
+        quant_act(3, 0)
+        quant_act(3, 1)
         rec_passes(0, 2)
-        turn_pair((3, 0), (3, 1))
-        quant_pair((3, 0), (3, 1))
         in_passes(0, 0)
-        in_passes(0, 1)
-        group_w(1, 0)
-        turn_pair((2, 2), (3, 2))
+        group_w_scalar(1, 0)
+        group_w_vector(1, 0)
+        decay(8)
+        turn_act(2, 2)
+        turn_act(3, 2)
+        unload_act(2, 2)
+        unload_act(3, 2)
         quant_w(1, 0)
-        quant_pair((2, 2), (3, 2))
-        group_w(1, 1)
+        quant_act(2, 2)
+        quant_act(3, 2)
+        group_w_vector(1, 1)
+        in_passes(0, 1)
+        rec_passes(0, 3)
         squash(0)
+        group_w_scalar(1, 1)
+        add_up(0)
         squash(1)
         quant_w(1, 1)
-        add_up(0)
-        rec_passes(0, 3)
         add_up(1)
         round_y(0, nc.scalar.copy)
 
@@ -348,7 +381,8 @@ def tile_leaky_recurrent_step_g4_kernel(tc, x, w_in, h, w_rec_words, w_rec_scale
             if k - 1 in group_at:
                 quant_w(*group_at[k - 1])
             if k in group_at:
-                group_w(*group_at[k])
+                group_w_scalar(*group_at[k])
+                group_w_vector(*group_at[k])
             if k - 1 >= ROUND_ON_VECTOR_FROM:
                 round_y(k - 1, nc.vector.tensor_copy)
             if k in planes_at:
@@ -357,18 +391,35 @@ def tile_leaky_recurrent_step_g4_kernel(tc, x, w_in, h, w_rec_words, w_rec_scale
         squash(14)
         turn_y(2, (0, 1))
         turn_y(2, (2, 3))
-        rec_passes(3, 3)
-        in_passes(3, 3)
+        half_bank = []
+        for half in range(2):
+            half_bank.append(psum.tile([P, N], F32, name="acc%d" % (3 * (1 - half))))
+            for quarter in range(2):
+                n0 = (2 * half + quarter) * P
+                out = half_bank[half][:, quarter * P : (quarter + 1) * P]
+                for g in range(4):
+                    rec_pass(3, 3, g, out, n0, n0 + P)
+                for g in range(2):
+                    in_pass(3, 3, g, out, n0, n0 + P)
         add_up(14)
         quant_y(2, (0, 1))
         round_y(14, nc.vector.tensor_copy)
         quant_y(2, (2, 3))
-        squash(15)
+        last_squashed = turn.tile([P, N], F32, name="squashed")
+        for half in range(2):
+            cols = slice(half * 256, (half + 1) * 256)
+            nc.scalar.activation(out=last_squashed[:, cols], in_=half_bank[half][:, :256], func=ACT.Tanh)
+            nc.vector.tensor_tensor(out=y[15][:, cols], in0=last_squashed[:, cols], in1=y[15][:, cols], op=ALU.add)
+        nc.sync.dma_start(out=out_0[3 * P :, 3 * N :], in_=y[15][:])
+        y_bf[15] = turn.tile([P, N], BF16, name="ybf", bufs=8, align_bytes=64)
+        for half in range(2):
+            nc.vector.tensor_copy(
+                out=y_bf[15][:].rearrange("r (u p e) -> r u p e", u=2, e=2)[:, :, half * 64 : (half + 1) * 64, :],
+                in_=y[15][:, half * 256 : (half + 1) * 256].rearrange("r (p u e) -> r u p e", u=2, e=2),
+            )
         turn_y(3, (0, 1))
         turn_y(3, (2,))
-        add_up(15)
         quant_y(3, (0, 1))
-        round_y(15, nc.vector.tensor_copy)
         quant_y(3, (2,))
         turn_y(3, (3,))
         quant_y(3, (3,))

@@ -18,10 +18,20 @@ ACT = mybir.ActivationFunctionType
 
 P = 128
 N = 512
+K_PASS = 512
+SLAB = 1024
+X_SLAB = 2
 TILES = B // P
 CHUNKS = H // N
+GROUPS = TILES * CHUNKS
+LAST = GROUPS - 1
+REC_PASSES = H // K_PASS
+IN_PASSES = D // K_PASS
+MX_ALIGN = 64
+TURN_BANKS = 4
+
 SCALAR_COLS = (256, 256, 128, 128)
-ROUND_ON_VECTOR_FROM = 12
+ROUND_ON_VECTOR_FROM = TILES * (CHUNKS - 1)
 
 
 def tile_leaky_recurrent_step_g4_kernel(tc, x, w_in, h, w_rec_words, w_rec_scales, leak, out_0, out_1, out_2):
@@ -33,398 +43,416 @@ def tile_leaky_recurrent_step_g4_kernel(tc, x, w_in, h, w_rec_words, w_rec_scale
 
     with ExitStack() as ctx:
         keep = ctx.enter_context(tc.tile_pool(name="keep", bufs=1))
-        turn = ctx.enter_context(tc.tile_pool(name="turn", bufs=4))
+        flow = ctx.enter_context(tc.tile_pool(name="flow", bufs=4))
         psum = ctx.enter_context(tc.psum_pool(name="psum", bufs=1))
         ctx.enter_context(tc.manual_schedule())
 
         ident = keep.tile([P, P], F32, name="ident")
         make_identity(nc, ident[:])
 
-        rs = []
+        r_scale = []
         for c in range(CHUNKS):
-            rs.append(keep.tile([P, 4, N], U8, name="rs%d" % c, align_bytes=64))
-            nc.vector.memset(rs[c][:].bitcast(I32), 0)
+            r_scale.append(keep.tile([P, REC_PASSES, N], U8, name="r_scale%d" % c, align_bytes=MX_ALIGN))
+            nc.vector.memset(r_scale[c][:].bitcast(I32), 0)
 
-        act = {}
+        h_raw = {}
         x_raw = {}
-        x_sorted = {}
-        rw = {}
         w_raw = {}
+        r_code = {}
 
-        def load_h(m, halves):
-            tile = keep.tile([P, len(halves) * 1024], BF16, name="h%d%d" % (m, halves[0]), align_bytes=64)
-            nc.sync.dma_start(out=tile[:], in_=h[m * P : (m + 1) * P, halves[0] * 1024 : (halves[-1] + 1) * 1024])
-            for i, j in enumerate(halves):
-                act[m, j] = tile[:, i * 1024 : (i + 1) * 1024]
+        def load_h(m, j0, j1):
+            tile = keep.tile([P, (j1 - j0) * SLAB], BF16, name="h%d%d" % (m, j0), align_bytes=MX_ALIGN)
+            nc.sync.dma_start(out=tile[:], in_=h[m * P : (m + 1) * P, j0 * SLAB : j1 * SLAB])
+            for j in range(j0, j1):
+                h_raw[m, j] = tile[:, (j - j0) * SLAB : (j - j0 + 1) * SLAB]
 
         def load_x(m):
-            tile = keep.tile([P, 2, D], BF16, name="x%d" % m, align_bytes=64)
-            nc.sync.dma_start(out=tile[:], in_=x[m * P : (m + 2) * P, :].rearrange("(i r) k -> r i k", i=2))
-            x_raw[m] = tile
+            x_raw[m] = keep.tile([P, 2, D], BF16, name="x%d" % m, align_bytes=MX_ALIGN)
+            nc.sync.dma_start(out=x_raw[m][:], in_=x[m * P : (m + 2) * P, :].rearrange("(i r) k -> r i k", i=2))
 
         def load_r_scales(c):
             for q in range(4):
                 nc.sync.dma_start(
-                    out=rs[c][32 * q : 32 * q + 4, :, :].bitcast(I32),
-                    in_=r_scales[:, 4 * q : 4 * q + 4, c * 128 : (c + 1) * 128].rearrange("g r n -> r g n"),
+                    out=r_scale[c][32 * q : 32 * q + 4, :, :].bitcast(I32),
+                    in_=r_scales[:, 4 * q : 4 * q + 4, c * N // 4 : (c + 1) * N // 4].rearrange("g r n -> r g n"),
                 )
 
         def load_r_words(c, g0, g1):
-            tile = keep.tile([P, g1 - g0, 2 * N], U8, name="rw%d%d" % (c, g0), align_bytes=64)
+            tile = keep.tile([P, g1 - g0, 2 * N], U8, name="r_code%d%d" % (c, g0), align_bytes=MX_ALIGN)
             nc.sync.dma_start(
                 out=tile[:].bitcast(I32),
-                in_=r_words[g0:g1, :, c * 256 : (c + 1) * 256].rearrange("g p n -> p g n"),
+                in_=r_words[g0:g1, :, c * N // 2 : (c + 1) * N // 2].rearrange("g p n -> p g n"),
             )
             for g in range(g0, g1):
-                rw[c, g] = tile[:, g - g0, :]
+                r_code[c, g] = tile[:, g - g0, :]
 
         def load_w(c, g):
-            w_raw[c, g] = keep.tile([P, 4, N], BF16, name="wraw%d%d" % (c, g), align_bytes=64)
+            w_raw[c, g] = keep.tile([P, 4, N], BF16, name="w_raw%d%d" % (c, g), align_bytes=MX_ALIGN)
             nc.sync.dma_start(
                 out=w_raw[c, g][:],
-                in_=w_in[g * 512 : (g + 1) * 512, c * N : (c + 1) * N].rearrange("(p t) n -> p t n", t=4),
+                in_=w_in[g * K_PASS : (g + 1) * K_PASS, c * N : (c + 1) * N].rearrange("(p t) n -> p t n", t=4),
             )
 
-        leak_rows = keep.tile([P, 16], BF16, name="leak_rows", align_bytes=64)
-        nc.sync.dma_start(out=leak_rows[:], in_=leak.rearrange("(q j) -> q j", j=16))
-        load_h(0, (0,))
-        load_h(0, (1,))
+        leak_rows = keep.tile([P, H // P], BF16, name="leak_rows", align_bytes=MX_ALIGN)
+        nc.sync.dma_start(out=leak_rows[:], in_=leak.rearrange("(q j) -> q j", q=P))
+        load_h(0, 0, 1)
+        load_h(0, 1, 2)
         load_r_scales(0)
         load_r_words(0, 0, 2)
         load_r_words(0, 2, 4)
-        load_h(1, (0, 1))
-        load_h(2, (0, 1))
+        load_h(1, 0, 2)
+        load_h(2, 0, 2)
         load_w(0, 0)
         load_x(0)
         load_w(0, 1)
-        load_h(3, (0, 1))
+        load_h(3, 0, 2)
         load_x(2)
         for c in range(1, CHUNKS):
             load_w(c, 0)
             load_w(c, 1)
             load_r_scales(c)
-            load_r_words(c, 0, 4)
+            load_r_words(c, 0, REC_PASSES)
 
-        turned = []
+        banks_taken = []
 
         def turn_bank():
-            bank = psum.tile([P, 2, 2, P], F32, name="tp%d" % (len(turned) % 4))
-            turned.append(bank)
+            bank = psum.tile([P, 2, 2, P], F32, name="turn%d" % (len(banks_taken) % TURN_BANKS))
+            banks_taken.append(bank)
             return bank
 
-        a_codes = {}
-        a_scales = {}
+        def grouped_tile():
+            return flow.tile([P, SLAB], BF16, name="grouped", align_bytes=MX_ALIGN, bufs=6)
 
-        a_bank = {}
-        a_grouped = {}
-
-        def sort_x(m):
-            tile = keep.tile([P, 4, 2, P], F32, name="xsorted%d" % m, align_bytes=64)
-            words = x_raw[m][:].rearrange("r i k -> r (i k)").bitcast(F32)
-            nc.vector.tensor_copy(out=tile[:], in_=words.rearrange("r (a p u) -> r a u p", a=4, u=2))
-            for i in range(2):
-                x_sorted[m + i] = tile[:, 2 * i : 2 * i + 2, :, :]
-
-        def turn_act(m, j):
-            a_bank[m, j] = turn_bank()
-            for g in range(2):
-                for u in range(2):
-                    if j == 2:
-                        src = x_sorted[m][:, g, u, :]
-                    else:
-                        src = act[m, j].bitcast(F32)[:, 256 * g + u : 256 * (g + 1) : 2]
-                    nc.tensor.transpose(a_bank[m, j][:, g, u, :], src, ident[:])
-
-        def unload_act(m, j, copy=nc.scalar.copy):
-            a_grouped[m, j] = turn.tile([P, 1024], BF16, name="grouped", align_bytes=64, bufs=6)
-            copy(
-                out=a_grouped[m, j][:].bitcast(F32).rearrange("p (g r u) -> p g r u", g=2, u=2),
-                in_=a_bank[m, j][:].rearrange("p g u r -> p g r u"),
-            )
-
-        def quant_act(m, j):
-            a_codes[m, j] = keep.tile([P, 256], U32, name="acodes%d%d" % (m, j), align_bytes=64)
-            a_scales[m, j] = keep.tile([P, 256], U8, name="ascales%d%d" % (m, j), align_bytes=64)
-            nc.vector.quantize_mx(out=a_codes[m, j][:].bitcast(FP8X4), scales=a_scales[m, j][:], in_=a_grouped[m, j][:])
-
-        leak_all = keep.tile([P, H], BF16, name="leak_all", align_bytes=64)
+        leak_all = keep.tile([P, H], BF16, name="leak_all", align_bytes=MX_ALIGN)
 
         def spread_leak(b):
-            words = leak_rows[:].bitcast(F32)
+            pairs = leak_rows[:].bitcast(F32)
             bank = turn_bank()
-            flat = bank[:].rearrange("p g u q -> p (g u) q")
+            blocks = bank[:].rearrange("p a b q -> p (a b) q")
             for j in range(4):
                 col = 4 * b + j
-                nc.tensor.transpose(flat[:, j, :], words[:, col : col + 1].to_broadcast([P, P]), ident[:])
+                nc.tensor.transpose(blocks[:, j, :], pairs[:, col : col + 1].to_broadcast([P, P]), ident[:])
             if b == 0:
                 nc.scalar.activation(
                     out=leak_all[:].rearrange("p (q j e) -> p q j e", j=8, e=2)[:, :, :4, :],
-                    in_=bank[:].rearrange("p g u q -> p (g u q)").bitcast(BF16).rearrange("p (j q e) -> p q j e", j=4, e=2),
+                    in_=bank[:].rearrange("p a b q -> p (a b q)").bitcast(BF16).rearrange("p (j q e) -> p q j e", j=4, e=2),
                     func=ACT.Copy,
                 )
             else:
                 nc.scalar.copy(
                     out=leak_all[:].bitcast(F32).rearrange("p (q j) -> p q j", j=8)[:, :, 4:],
-                    in_=flat.rearrange("p j q -> p q j"),
+                    in_=blocks.rearrange("p j q -> p q j"),
                 )
 
-        w_codes = {}
-        w_scales = {}
-        w_grouped = {}
+        x_sorted = {}
+        slab_bank = {}
+        slab_grouped = {}
+        a_code = {}
+        a_scale = {}
 
-        def group_w(c, g, copy, cols):
+        def sort_x(m):
+            tile = keep.tile([P, 2 * IN_PASSES, 2, P], F32, name="x_sorted%d" % m, align_bytes=MX_ALIGN)
+            pairs = x_raw[m][:].rearrange("r i k -> r (i k)").bitcast(F32)
+            nc.vector.tensor_copy(out=tile[:], in_=pairs.rearrange("r (a p u) -> r a u p", a=2 * IN_PASSES, u=2))
+            for i in range(2):
+                x_sorted[m + i] = tile[:, IN_PASSES * i : IN_PASSES * (i + 1), :, :]
+
+        def turn_slab(m, j):
+            slab_bank[m, j] = turn_bank()
+            for g in range(2):
+                for u in range(2):
+                    if j == X_SLAB:
+                        pairs = x_sorted[m][:, g, u, :]
+                    else:
+                        pairs = h_raw[m, j].bitcast(F32)[:, 2 * P * g + u : 2 * P * (g + 1) : 2]
+                    nc.tensor.transpose(slab_bank[m, j][:, g, u, :], pairs, ident[:])
+
+        def unload_slab(m, j, copy=nc.scalar.copy):
+            slab_grouped[m, j] = grouped_tile()
+            copy(
+                out=slab_grouped[m, j][:].bitcast(F32).rearrange("p (g r u) -> p g r u", g=2, u=2),
+                in_=slab_bank[m, j][:].rearrange("p g u r -> p g r u"),
+            )
+
+        def quant_slab(m, j):
+            a_code[m, j] = keep.tile([P, 2 * P], U32, name="a_code%d%d" % (m, j), align_bytes=MX_ALIGN)
+            a_scale[m, j] = keep.tile([P, 2 * P], U8, name="a_scale%d%d" % (m, j), align_bytes=MX_ALIGN)
+            nc.vector.quantize_mx(out=a_code[m, j][:].bitcast(FP8X4), scales=a_scale[m, j][:], in_=slab_grouped[m, j][:])
+
+        w_grouped = {}
+        w_code = {}
+        w_scale = {}
+
+        def regroup_w(c, g, copy, cols):
             if (c, g) not in w_grouped:
-                w_grouped[c, g] = turn.tile([P, N, 4], BF16, name="wi", align_bytes=64, bufs=3)
+                w_grouped[c, g] = flow.tile([P, N, 4], BF16, name="w_grouped", align_bytes=MX_ALIGN, bufs=3)
             copy(
                 out=w_grouped[c, g][:, cols, :].rearrange("p (n i) t -> p n t i", i=4),
                 in_=w_raw[c, g][:, :, cols].rearrange("p t (n i) -> p n t i", i=4),
             )
 
-        def group_w_scalar(c, g):
-            group_w(c, g, nc.scalar.copy, slice(0, SCALAR_COLS[c]))
+        def regroup_w_scalar(c, g):
+            regroup_w(c, g, nc.scalar.copy, slice(0, SCALAR_COLS[c]))
 
-        def group_w_vector(c, g):
-            group_w(c, g, nc.vector.tensor_copy, slice(SCALAR_COLS[c], N))
+        def regroup_w_vector(c, g):
+            regroup_w(c, g, nc.vector.tensor_copy, slice(SCALAR_COLS[c], N))
 
         def quant_w(c, g):
-            w_codes[c, g] = keep.tile([P, N], U32, name="wcodes%d%d" % (c, g), align_bytes=64)
-            w_scales[c, g] = keep.tile([P, N], U8, name="wscales%d%d" % (c, g), align_bytes=64)
+            w_code[c, g] = keep.tile([P, N], U32, name="w_code%d%d" % (c, g), align_bytes=MX_ALIGN)
+            w_scale[c, g] = keep.tile([P, N], U8, name="w_scale%d%d" % (c, g), align_bytes=MX_ALIGN)
             nc.vector.quantize_mx(
-                out=w_codes[c, g][:].bitcast(FP8X4),
-                scales=w_scales[c, g][:],
+                out=w_code[c, g][:].bitcast(FP8X4),
+                scales=w_scale[c, g][:],
                 in_=w_grouped[c, g][:].rearrange("p n t -> p (n t)"),
             )
 
-        acc = {}
+        drive = {}
 
-        def rec_pass(c, m, g, out, n0, n1):
-            j, cols = g // 2, slice((g % 2) * P, (g % 2 + 1) * P)
+        def drive_bank(m):
+            return psum.tile([P, N], F32, name="drive%d" % m)
+
+        def rec_pass(group, g, out, n0, n1):
+            c, m = divmod(group, TILES)
+            j, rows = g // 2, slice((g % 2) * P, (g % 2 + 1) * P)
             nc.tensor.matmul_mx(
                 out=out,
-                lhsT=a_codes[m, j][:, cols].bitcast(FP8X4),
-                lhsT_scale=a_scales[m, j][:, cols],
-                rhs=rw[c, g][:, 2 * n0 : 2 * n1].bitcast(FP4X4),
-                rhs_scale=rs[c][:, g, n0:n1],
+                lhsT=a_code[m, j][:, rows].bitcast(FP8X4),
+                lhsT_scale=a_scale[m, j][:, rows],
+                rhs=r_code[c, g][:, 2 * n0 : 2 * n1].bitcast(FP4X4),
+                rhs_scale=r_scale[c][:, g, n0:n1],
                 start=(g == 0),
                 stop=False,
             )
 
-        def in_pass(c, m, g, out, n0, n1):
-            cols = slice(g * P, (g + 1) * P)
+        def in_pass(group, g, out, n0, n1):
+            c, m = divmod(group, TILES)
+            rows = slice(g * P, (g + 1) * P)
             nc.tensor.matmul_mx(
                 out=out,
-                lhsT=a_codes[m, 2][:, cols].bitcast(FP8X4),
-                lhsT_scale=a_scales[m, 2][:, cols],
-                rhs=w_codes[c, g][:, n0:n1].bitcast(FP8X4),
-                rhs_scale=w_scales[c, g][:, n0:n1],
+                lhsT=a_code[m, X_SLAB][:, rows].bitcast(FP8X4),
+                lhsT_scale=a_scale[m, X_SLAB][:, rows],
+                rhs=w_code[c, g][:, n0:n1].bitcast(FP8X4),
+                rhs_scale=w_scale[c, g][:, n0:n1],
                 start=False,
-                stop=(g == 1),
+                stop=(g == IN_PASSES - 1),
             )
 
-        def rec_passes(c, m, g0=0, g1=4):
+        def rec_passes(group, g0=0, g1=REC_PASSES):
             if g0 == 0:
-                acc[c, m] = psum.tile([P, N], F32, name="acc%d" % m)
+                drive[group] = drive_bank(group % TILES)
             for g in range(g0, g1):
-                rec_pass(c, m, g, acc[c, m][:], 0, N)
+                rec_pass(group, g, drive[group][:], 0, N)
 
-        def in_passes(c, m):
-            for g in range(2):
-                in_pass(c, m, g, acc[c, m][:], 0, N)
+        def in_passes(group):
+            for g in range(IN_PASSES):
+                in_pass(group, g, drive[group][:], 0, N)
 
         y = {}
         y_bf = {}
         squashed = {}
 
-        def decay(k):
-            c, m = divmod(k, TILES)
-            y[k] = keep.tile([P, N], F32, name="y%d" % k)
-            h_cols = slice((c % 2) * N, (c % 2 + 1) * N)
-            nc.vector.tensor_tensor(out=y[k][:], in0=act[m, c // 2][:, h_cols], in1=leak_all[:, c * N : (c + 1) * N], op=ALU.mult)
+        def decay(group):
+            c, m = divmod(group, TILES)
+            y[group] = keep.tile([P, N], F32, name="y%d" % group)
+            old = h_raw[m, c // 2][:, (c % 2) * N : (c % 2 + 1) * N]
+            nc.vector.tensor_tensor(out=y[group][:], in0=old, in1=leak_all[:, c * N : (c + 1) * N], op=ALU.mult)
 
-        def squash(k):
-            squashed[k] = turn.tile([P, N], F32, name="squashed")
-            nc.scalar.activation(out=squashed[k][:], in_=acc[divmod(k, TILES)][:], func=ACT.Tanh)
+        def squashed_tile():
+            return flow.tile([P, N], F32, name="squashed")
 
-        def add_up(k):
-            c, m = divmod(k, TILES)
-            nc.vector.tensor_tensor(out=y[k][:], in0=squashed[k][:], in1=y[k][:], op=ALU.add)
-            nc.sync.dma_start(out=out_0[m * P : (m + 1) * P, c * N : (c + 1) * N], in_=y[k][:])
+        def rounded_tile():
+            return flow.tile([P, N], BF16, name="y_bf", bufs=8, align_bytes=MX_ALIGN)
 
-        def round_y(k, copy):
-            y_bf[k] = turn.tile([P, N], BF16, name="ybf", bufs=8, align_bytes=64)
+        def squash(group):
+            squashed[group] = squashed_tile()
+            nc.scalar.activation(out=squashed[group][:], in_=drive[group][:], func=ACT.Tanh)
+
+        def store_y(group):
+            c, m = divmod(group, TILES)
+            nc.sync.dma_start(out=out_0[m * P : (m + 1) * P, c * N : (c + 1) * N], in_=y[group][:])
+
+        def add_up(group):
+            nc.vector.tensor_tensor(out=y[group][:], in0=squashed[group][:], in1=y[group][:], op=ALU.add)
+            store_y(group)
+
+        def round_y(group, copy):
+            y_bf[group] = rounded_tile()
             copy(
-                out=y_bf[k][:].rearrange("r (u p e) -> r u p e", u=2, e=2),
-                in_=y[k][:].rearrange("r (p u e) -> r u p e", u=2, e=2),
+                out=y_bf[group][:].rearrange("r (u p e) -> r u p e", u=2, e=2),
+                in_=y[group][:].rearrange("r (p u e) -> r u p e", u=2, e=2),
             )
 
-        plane_scales = keep.tile([P, B], U8, name="plane_scales", align_bytes=64)
-        plane_codes = []
+        y_scale = keep.tile([P, B], U8, name="y_scale", align_bytes=MX_ALIGN)
+        y_code = []
         for c in range(CHUNKS):
-            plane_codes.append(keep.tile([P, B], U32, name="plane_codes%d" % c, align_bytes=64))
-
+            y_code.append(keep.tile([P, B], U32, name="y_code%d" % c, align_bytes=MX_ALIGN))
         y_grouped = {}
 
-        def turn_y(c, ms):
-            n = len(ms)
+        def turn_y(c, m0, m1):
+            n = m1 - m0
             bank = turn_bank()
-            for i, m in enumerate(ms):
-                words = y_bf[TILES * c + m][:].bitcast(F32)
+            for i in range(n):
+                pairs = y_bf[TILES * c + m0 + i][:].bitcast(F32)
                 for u in range(2):
-                    nc.tensor.transpose(bank[:, i, u, :], words[:, u * P : (u + 1) * P], ident[:])
-            y_grouped[c, ms] = turn.tile([P, 1024], BF16, name="grouped", align_bytes=64, bufs=6)
+                    nc.tensor.transpose(bank[:, i, u, :], pairs[:, u * P : (u + 1) * P], ident[:])
+            y_grouped[c, m0] = grouped_tile()
             nc.scalar.copy(
-                out=y_grouped[c, ms][:, : n * 512].bitcast(F32).rearrange("p (i r u) -> p i r u", i=n, u=2),
+                out=y_grouped[c, m0][:, : n * N].bitcast(F32).rearrange("p (i r u) -> p i r u", i=n, u=2),
                 in_=bank[:, :n, :, :].rearrange("p i u r -> p i r u"),
             )
 
-        def quant_y(c, ms):
-            n = len(ms)
-            cols = slice(ms[0] * P, (ms[0] + n) * P)
+        def quant_y(c, m0, m1):
+            rows = slice(m0 * P, m1 * P)
             nc.vector.quantize_mx(
-                out=plane_codes[c][:, cols].bitcast(FP8X4),
-                scales=plane_scales[4 * c :, cols],
-                in_=y_grouped[c, ms][:, : n * 512],
+                out=y_code[c][:, rows].bitcast(FP8X4),
+                scales=y_scale[4 * c :, rows],
+                in_=y_grouped[c, m0][:, : (m1 - m0) * N],
             )
-            nc.sync.dma_start(out=y_words[c, :, cols], in_=plane_codes[c][:, cols].bitcast(I32))
+            nc.sync.dma_start(out=y_words[c, :, rows], in_=y_code[c][:, rows].bitcast(I32))
+
 
         spread_leak(0)
-        turn_act(0, 0)
-        unload_act(0, 0, nc.vector.tensor_copy)
-        quant_act(0, 0)
-        turn_act(0, 1)
-        unload_act(0, 1)
+        turn_slab(0, 0)
+        unload_slab(0, 0, nc.vector.tensor_copy)
+        quant_slab(0, 0)
+        turn_slab(0, 1)
+        unload_slab(0, 1)
         spread_leak(1)
-        quant_act(0, 1)
-        rec_passes(0, 0, 0, 2)
-        decay(0)
-        decay(4)
-        turn_act(1, 0)
-        unload_act(1, 0)
-        decay(1)
-        decay(5)
-        group_w_vector(0, 0)
-        group_w_scalar(0, 0)
-        turn_act(1, 1)
-        quant_act(1, 0)
+        quant_slab(0, 1)
+        rec_passes(0, 0, 2)
+
+        turn_slab(1, 0)
+        turn_slab(1, 1)
+        unload_slab(1, 0)
+        regroup_w_scalar(0, 0)
+        unload_slab(1, 1)
+        for m in range(2):
+            decay(m)
+            decay(TILES + m)
+        regroup_w_vector(0, 0)
+        quant_slab(1, 0)
         sort_x(0)
-        unload_act(1, 1)
-        rec_passes(0, 0, 2, 4)
+        quant_slab(1, 1)
+        rec_passes(0, 2, 4)
+
+        def turn_run(run):
+            for m, j in run:
+                turn_slab(m, j)
+            for m, j in run:
+                unload_slab(m, j)
+
+        def quant_run(run):
+            for m, j in run:
+                quant_slab(m, j)
+
+        run = ((2, 0), (2, 1), (0, X_SLAB))
+        turn_run(run)
+        regroup_w_scalar(0, 1)
         decay(2)
         quant_w(0, 0)
-        turn_act(2, 0)
-        turn_act(2, 1)
-        turn_act(0, 2)
-        unload_act(2, 0)
-        unload_act(2, 1)
-        unload_act(0, 2)
-        quant_act(1, 1)
-        quant_act(2, 0)
-        group_w_vector(0, 1)
-        quant_act(2, 1)
-        quant_act(0, 2)
-        rec_passes(0, 1)
-        group_w_scalar(0, 1)
+        regroup_w_vector(0, 1)
+        quant_run(run)
         sort_x(2)
-        turn_act(1, 2)
-        turn_act(3, 0)
-        turn_act(3, 1)
-        unload_act(1, 2)
-        unload_act(3, 0)
-        unload_act(3, 1)
-        quant_w(0, 1)
-        quant_act(1, 2)
+        rec_passes(1)
+
+        run = ((1, X_SLAB), (3, 0), (3, 1))
+        turn_run(run)
+        regroup_w_scalar(1, 0)
         decay(3)
-        quant_act(3, 0)
-        quant_act(3, 1)
-        rec_passes(0, 2)
-        in_passes(0, 0)
-        group_w_scalar(1, 0)
-        group_w_vector(1, 0)
-        decay(8)
-        turn_act(2, 2)
-        turn_act(3, 2)
-        unload_act(2, 2)
-        unload_act(3, 2)
-        quant_w(1, 0)
-        quant_act(2, 2)
-        quant_act(3, 2)
-        group_w_vector(1, 1)
-        in_passes(0, 1)
-        rec_passes(0, 3)
+        quant_w(0, 1)
+        quant_run(run)
+        regroup_w_vector(1, 0)
+        rec_passes(2)
+        in_passes(0)
+
+        run = ((2, X_SLAB), (3, X_SLAB))
+        turn_run(run)
         squash(0)
-        group_w_scalar(1, 1)
+        regroup_w_scalar(1, 1)
+        decay(TILES + 2)
+        quant_w(1, 0)
+        quant_run(run)
+        regroup_w_vector(1, 1)
+        in_passes(1)
+        rec_passes(3)
         add_up(0)
         squash(1)
         quant_w(1, 1)
         add_up(1)
         round_y(0, nc.scalar.copy)
 
-        decay_at = {2: 6, 3: 7, 6: 9, 7: 10, 9: 11, 10: 12, 11: 13, 12: 14, 13: 15}
-        group_at = {3: (2, 0), 5: (2, 1), 7: (3, 0), 9: (3, 1)}
-        planes_at = {7: 0, 11: 1}
-        for k in range(2, 15):
-            c, m = divmod(k, TILES)
-            if c > 0:
-                rec_passes(c, m)
-            in_passes(c, m)
-            if k >= 3:
-                squash(k - 1)
-                if k - 2 < ROUND_ON_VECTOR_FROM:
-                    round_y(k - 2, nc.scalar.copy)
-            if k in planes_at:
-                turn_y(planes_at[k], (0, 1))
-                turn_y(planes_at[k], (2, 3))
-            if k in decay_at:
-                decay(decay_at[k])
-            if k >= 3:
-                add_up(k - 1)
-            if k - 1 in group_at:
-                quant_w(*group_at[k - 1])
-            if k in group_at:
-                group_w_scalar(*group_at[k])
-                group_w_vector(*group_at[k])
-            if k - 1 >= ROUND_ON_VECTOR_FROM:
-                round_y(k - 1, nc.vector.tensor_copy)
-            if k in planes_at:
-                quant_y(planes_at[k], (0, 1))
-                quant_y(planes_at[k], (2, 3))
-        squash(14)
-        turn_y(2, (0, 1))
-        turn_y(2, (2, 3))
+        first_step = 2
+        regroup_at = {3 + 2 * i: (2 + i // IN_PASSES, i % IN_PASSES) for i in range(2 * IN_PASSES)}
+        to_decay = list(range(TILES + 3, GROUPS))
+        for s in range(first_step, LAST):
+            if s >= TILES:
+                rec_passes(s)
+            in_passes(s)
+            if s > first_step:
+                squash(s - 1)
+                if s - 2 < ROUND_ON_VECTOR_FROM:
+                    round_y(s - 2, nc.scalar.copy)
+            ready = s // TILES - 1 if s > TILES and s % TILES == TILES - 1 else None
+            if ready is not None:
+                turn_y(ready, 0, 2)
+                turn_y(ready, 2, 4)
+            steps_left = LAST - 1 - s
+            if to_decay and (s - 1 not in regroup_at or steps_left <= len(to_decay)):
+                decay(to_decay[0])
+                to_decay = to_decay[1:]
+            if s > first_step:
+                add_up(s - 1)
+            if s - 1 in regroup_at:
+                quant_w(*regroup_at[s - 1])
+            if s in regroup_at:
+                regroup_w_scalar(*regroup_at[s])
+                regroup_w_vector(*regroup_at[s])
+            if s - 1 >= ROUND_ON_VECTOR_FROM:
+                round_y(s - 1, nc.vector.tensor_copy)
+            if ready is not None:
+                quant_y(ready, 0, 2)
+                quant_y(ready, 2, 4)
+
+        squash(LAST - 1)
+        turn_y(CHUNKS - 2, 0, 2)
+        turn_y(CHUNKS - 2, 2, 4)
+
+        half = N // 2
         half_bank = []
-        for half in range(2):
-            half_bank.append(psum.tile([P, N], F32, name="acc%d" % (3 * (1 - half))))
+        for a, m in enumerate((TILES - 1, 0)):
+            half_bank.append(drive_bank(m))
             for quarter in range(2):
-                n0 = (2 * half + quarter) * P
-                out = half_bank[half][:, quarter * P : (quarter + 1) * P]
-                for g in range(4):
-                    rec_pass(3, 3, g, out, n0, n0 + P)
-                for g in range(2):
-                    in_pass(3, 3, g, out, n0, n0 + P)
-        add_up(14)
-        quant_y(2, (0, 1))
-        round_y(14, nc.vector.tensor_copy)
-        quant_y(2, (2, 3))
-        last_squashed = turn.tile([P, N], F32, name="squashed")
-        for half in range(2):
-            cols = slice(half * 256, (half + 1) * 256)
-            nc.scalar.activation(out=last_squashed[:, cols], in_=half_bank[half][:, :256], func=ACT.Tanh)
-            nc.vector.tensor_tensor(out=y[15][:, cols], in0=last_squashed[:, cols], in1=y[15][:, cols], op=ALU.add)
-        nc.sync.dma_start(out=out_0[3 * P :, 3 * N :], in_=y[15][:])
-        y_bf[15] = turn.tile([P, N], BF16, name="ybf", bufs=8, align_bytes=64)
-        for half in range(2):
+                n0 = a * half + quarter * P
+                out = half_bank[a][:, quarter * P : (quarter + 1) * P]
+                for g in range(REC_PASSES):
+                    rec_pass(LAST, g, out, n0, n0 + P)
+                for g in range(IN_PASSES):
+                    in_pass(LAST, g, out, n0, n0 + P)
+        add_up(LAST - 1)
+        quant_y(CHUNKS - 2, 0, 2)
+        round_y(LAST - 1, nc.vector.tensor_copy)
+        quant_y(CHUNKS - 2, 2, 4)
+
+        squashed[LAST] = squashed_tile()
+        for a in range(2):
+            cols = slice(a * half, (a + 1) * half)
+            nc.scalar.activation(out=squashed[LAST][:, cols], in_=half_bank[a][:, :half], func=ACT.Tanh)
+            nc.vector.tensor_tensor(out=y[LAST][:, cols], in0=squashed[LAST][:, cols], in1=y[LAST][:, cols], op=ALU.add)
+        store_y(LAST)
+        y_bf[LAST] = rounded_tile()
+        for a in range(2):
             nc.vector.tensor_copy(
-                out=y_bf[15][:].rearrange("r (u p e) -> r u p e", u=2, e=2)[:, :, half * 64 : (half + 1) * 64, :],
-                in_=y[15][:, half * 256 : (half + 1) * 256].rearrange("r (p u e) -> r u p e", u=2, e=2),
+                out=y_bf[LAST][:].rearrange("r (u p e) -> r u p e", u=2, e=2)[:, :, a * P // 2 : (a + 1) * P // 2, :],
+                in_=y[LAST][:, a * half : (a + 1) * half].rearrange("r (p u e) -> r u p e", u=2, e=2),
             )
-        turn_y(3, (0, 1))
-        turn_y(3, (2,))
-        quant_y(3, (0, 1))
-        quant_y(3, (2,))
-        turn_y(3, (3,))
-        quant_y(3, (3,))
+
+        turn_y(CHUNKS - 1, 0, 2)
+        turn_y(CHUNKS - 1, 2, 3)
+        quant_y(CHUNKS - 1, 0, 2)
+        quant_y(CHUNKS - 1, 2, 3)
+        turn_y(CHUNKS - 1, 3, 4)
+        quant_y(CHUNKS - 1, 3, 4)
+
         for q in range(4):
-            eng = nc.sync if q < 2 else nc.scalar
-            eng.dma_start(
-                out=y_scales[:, 4 * q : 4 * q + 4, :], in_=plane_scales[32 * q : 32 * q + 16, :].bitcast(I32)
-            )
+            queue = nc.sync if q < 2 else nc.scalar
+            queue.dma_start(out=y_scales[:, 4 * q : 4 * q + 4, :], in_=y_scale[32 * q : 32 * q + 16, :].bitcast(I32))

@@ -55,6 +55,7 @@ def tile_leaky_recurrent_step_g4_kernel(tc, x, w_in, h, w_rec_words, w_rec_scale
             r_scale.append(keep.tile([P, REC_PASSES, N], U8, name="r_scale%d" % c, align_bytes=MX_ALIGN))
             nc.vector.memset(r_scale[c][:].bitcast(I32), 0)
 
+        h_rows = {}
         h_raw = {}
         x_raw = {}
         w_raw = {}
@@ -63,6 +64,7 @@ def tile_leaky_recurrent_step_g4_kernel(tc, x, w_in, h, w_rec_words, w_rec_scale
         def load_h(m, j0, j1):
             tile = keep.tile([P, (j1 - j0) * SLAB], BF16, name="h%d%d" % (m, j0), align_bytes=MX_ALIGN)
             nc.sync.dma_start(out=tile[:], in_=h[m * P : (m + 1) * P, j0 * SLAB : j1 * SLAB])
+            h_rows[m] = tile
             for j in range(j0, j1):
                 h_raw[m, j] = tile[:, (j - j0) * SLAB : (j - j0 + 1) * SLAB]
 
@@ -144,25 +146,30 @@ def tile_leaky_recurrent_step_g4_kernel(tc, x, w_in, h, w_rec_words, w_rec_scale
                     in_=blocks.rearrange("p j q -> p q j"),
                 )
 
-        x_sorted = {}
+        slab_sorted = {}
         slab_bank = {}
         slab_grouped = {}
         a_code = {}
         a_scale = {}
 
+        def sort_slabs(raw, slabs):
+            tile = keep.tile([P, 4, 2, P], F32, name="sorted%d%d" % slabs[0], align_bytes=MX_ALIGN)
+            nc.vector.tensor_copy(out=tile[:], in_=raw.bitcast(F32).rearrange("r (a p u) -> r a u p", a=4, u=2))
+            for i, slab in enumerate(slabs):
+                slab_sorted[slab] = tile[:, 2 * i : 2 * i + 2, :, :]
+
         def sort_x(m):
-            tile = keep.tile([P, 2 * IN_PASSES, 2, P], F32, name="x_sorted%d" % m, align_bytes=MX_ALIGN)
-            pairs = x_raw[m][:].rearrange("r i k -> r (i k)").bitcast(F32)
-            nc.vector.tensor_copy(out=tile[:], in_=pairs.rearrange("r (a p u) -> r a u p", a=2 * IN_PASSES, u=2))
-            for i in range(2):
-                x_sorted[m + i] = tile[:, IN_PASSES * i : IN_PASSES * (i + 1), :, :]
+            sort_slabs(x_raw[m][:].rearrange("r i k -> r (i k)"), ((m, X_SLAB), (m + 1, X_SLAB)))
+
+        def sort_h(m):
+            sort_slabs(h_rows[m][:], ((m, 0), (m, 1)))
 
         def turn_slab(m, j):
             slab_bank[m, j] = turn_bank()
             for g in range(2):
                 for u in range(2):
-                    if j == X_SLAB:
-                        pairs = x_sorted[m][:, g, u, :]
+                    if (m, j) in slab_sorted:
+                        pairs = slab_sorted[m, j][:, g, u, :]
                     else:
                         pairs = h_raw[m, j].bitcast(F32)[:, 2 * P * g + u : 2 * P * (g + 1) : 2]
                     nc.tensor.transpose(slab_bank[m, j][:, g, u, :], pairs, ident[:])
@@ -329,6 +336,7 @@ def tile_leaky_recurrent_step_g4_kernel(tc, x, w_in, h, w_rec_words, w_rec_scale
         for m in range(2):
             decay(m)
             decay(TILES + m)
+        sort_h(2)
         regroup_w_vector(0, 0)
         quant_slab(1, 0)
         sort_x(0)
@@ -390,8 +398,7 @@ def tile_leaky_recurrent_step_g4_kernel(tc, x, w_in, h, w_rec_words, w_rec_scale
             in_passes(s)
             if s > first_step:
                 squash(s - 1)
-                if s - 2 < ROUND_ON_VECTOR_FROM:
-                    round_y(s - 2, nc.scalar.copy)
+                round_y(s - 2, nc.scalar.copy if s - 2 < ROUND_ON_VECTOR_FROM else nc.vector.tensor_copy)
             ready = s // TILES - 1 if s > TILES and s % TILES == TILES - 1 else None
             if ready is not None:
                 turn_y(ready, 0, 2)
@@ -407,8 +414,6 @@ def tile_leaky_recurrent_step_g4_kernel(tc, x, w_in, h, w_rec_words, w_rec_scale
             if s in regroup_at:
                 regroup_w_scalar(*regroup_at[s])
                 regroup_w_vector(*regroup_at[s])
-            if s - 1 >= ROUND_ON_VECTOR_FROM:
-                round_y(s - 1, nc.vector.tensor_copy)
             if ready is not None:
                 quant_y(ready, 0, 2)
                 quant_y(ready, 2, 4)
@@ -428,6 +433,7 @@ def tile_leaky_recurrent_step_g4_kernel(tc, x, w_in, h, w_rec_words, w_rec_scale
                     rec_pass(LAST, g, out, n0, n0 + P)
                 for g in range(IN_PASSES):
                     in_pass(LAST, g, out, n0, n0 + P)
+        round_y(LAST - 2, nc.vector.tensor_copy)
         add_up(LAST - 1)
         quant_y(CHUNKS - 2, 0, 2)
         round_y(LAST - 1, nc.vector.tensor_copy)

from contextlib import ExitStack

import concourse.mybir as mybir
from concourse.masks import make_identity

B, D, H = 512, 1024, 2048
FLOPS = 2 * B * (D + H) * H

F32 = mybir.dt.float32
BF16 = mybir.dt.bfloat16
I32 = mybir.dt.int32
U32 = mybir.dt.uint32
U8 = mybir.dt.uint8
FP8X4 = mybir.dt.float8_e4m3fn_x4
FP4X4 = mybir.dt.float4_e2m1fn_x4
ALU = mybir.AluOpType
ACT = mybir.ActivationFunctionType

P = 128
N = 512
K_PASS = 512
SLAB = 1024
X_SLAB = 2
TILES = B // P
CHUNKS = H // N
GROUPS = TILES * CHUNKS
LAST = GROUPS - 1
REC_PASSES = H // K_PASS
IN_PASSES = D // K_PASS
MX_ALIGN = 64
TURN_BANKS = 4

SCALAR_COLS = (256, 256, 128, 128)
ROUND_ON_VECTOR_FROM = TILES * (CHUNKS - 1)


def tile_leaky_recurrent_step_g4_kernel(tc, x, w_in, h, w_rec_words, w_rec_scales, leak, out_0, out_1, out_2):
    nc = tc.nc
    r_words = w_rec_words.bitcast(I32)
    r_scales = w_rec_scales.bitcast(I32)
    y_words = out_1.rearrange("g p m t -> g p (m t)").bitcast(I32)
    y_scales = out_2.bitcast(I32)

    with ExitStack() as ctx:
        keep = ctx.enter_context(tc.tile_pool(name="keep", bufs=1))
        flow = ctx.enter_context(tc.tile_pool(name="flow", bufs=4))
        psum = ctx.enter_context(tc.psum_pool(name="psum", bufs=1))
        ctx.enter_context(tc.manual_schedule())

        ident = keep.tile([P, P], F32, name="ident")
        make_identity(nc, ident[:])

        r_scale = []
        for c in range(CHUNKS):
            r_scale.append(keep.tile([P, REC_PASSES, N], U8, name="r_scale%d" % c, align_bytes=MX_ALIGN))
            nc.vector.memset(r_scale[c][:].bitcast(I32), 0)

        h_rows = {}
        h_raw = {}
        x_raw = {}
        w_raw = {}
        r_code = {}

        def load_h(m, j0, j1):
            tile = keep.tile([P, (j1 - j0) * SLAB], BF16, name="h%d%d" % (m, j0), align_bytes=MX_ALIGN)
            nc.sync.dma_start(out=tile[:], in_=h[m * P : (m + 1) * P, j0 * SLAB : j1 * SLAB])
            h_rows[m] = tile
            for j in range(j0, j1):
                h_raw[m, j] = tile[:, (j - j0) * SLAB : (j - j0 + 1) * SLAB]

        def load_x(m):
            x_raw[m] = keep.tile([P, 2, D], BF16, name="x%d" % m, align_bytes=MX_ALIGN)
            nc.sync.dma_start(out=x_raw[m][:], in_=x[m * P : (m + 2) * P, :].rearrange("(i r) k -> r i k", i=2))

        def load_r_scales(c):
            for q in range(4):
                nc.sync.dma_start(
                    out=r_scale[c][32 * q : 32 * q + 4, :, :].bitcast(I32),
                    in_=r_scales[:, 4 * q : 4 * q + 4, c * N // 4 : (c + 1) * N // 4].rearrange("g r n -> r g n"),
                )

        def load_r_words(c, g0, g1):
            tile = keep.tile([P, g1 - g0, 2 * N], U8, name="r_code%d%d" % (c, g0), align_bytes=MX_ALIGN)
            nc.sync.dma_start(
                out=tile[:].bitcast(I32),
                in_=r_words[g0:g1, :, c * N // 2 : (c + 1) * N // 2].rearrange("g p n -> p g n"),
            )
            for g in range(g0, g1):
                r_code[c, g] = tile[:, g - g0, :]

        def load_w(c, g):
            w_raw[c, g] = keep.tile([P, 4, N], BF16, name="w_raw%d%d" % (c, g), align_bytes=MX_ALIGN)
            nc.sync.dma_start(
                out=w_raw[c, g][:],
                in_=w_in[g * K_PASS : (g + 1) * K_PASS, c * N : (c + 1) * N].rearrange("(p t) n -> p t n", t=4),
            )

        leak_rows = keep.tile([P, H // P], BF16, name="leak_rows", align_bytes=MX_ALIGN)
        nc.sync.dma_start(out=leak_rows[:], in_=leak.rearrange("(q j) -> q j", q=P))
        load_h(0, 0, 1)
        load_h(0, 1, 2)
        load_r_scales(0)
        load_r_words(0, 0, 2)
        load_r_words(0, 2, 4)
        load_h(1, 0, 2)
        load_h(2, 0, 2)
        load_w(0, 0)
        load_x(0)
        load_w(0, 1)
        load_h(3, 0, 2)
        load_x(2)
        for c in range(1, CHUNKS):
            load_w(c, 0)
            load_w(c, 1)
            load_r_scales(c)
            load_r_words(c, 0, REC_PASSES)

        banks_taken = []

        def turn_bank():
            bank = psum.tile([P, 2, 2, P], F32, name="turn%d" % (len(banks_taken) % TURN_BANKS))
            banks_taken.append(bank)
            return bank

        def grouped_tile():
            return flow.tile([P, SLAB], BF16, name="grouped", align_bytes=MX_ALIGN, bufs=6)

        leak_all = keep.tile([P, H], BF16, name="leak_all", align_bytes=MX_ALIGN)

        def spread_leak(b):
            pairs = leak_rows[:].bitcast(F32)
            bank = turn_bank()
            blocks = bank[:].rearrange("p a b q -> p (a b) q")
            for j in range(4):
                col = 4 * b + j
                nc.tensor.transpose(blocks[:, j, :], pairs[:, col : col + 1].to_broadcast([P, P]), ident[:])
            if b == 0:
                nc.scalar.activation(
                    out=leak_all[:].rearrange("p (q j e) -> p q j e", j=8, e=2)[:, :, :4, :],
                    in_=bank[:].rearrange("p a b q -> p (a b q)").bitcast(BF16).rearrange("p (j q e) -> p q j e", j=4, e=2),
                    func=ACT.Copy,
                )
            else:
                nc.scalar.copy(
                    out=leak_all[:].bitcast(F32).rearrange("p (q j) -> p q j", j=8)[:, :, 4:],
                    in_=blocks.rearrange("p j q -> p q j"),
                )

        slab_sorted = {}
        slab_bank = {}
        slab_grouped = {}
        a_code = {}
        a_scale = {}

        def sort_slabs(raw, slabs):
            tile = keep.tile([P, 4, 2, P], F32, name="sorted%d%d" % slabs[0], align_bytes=MX_ALIGN)
            nc.vector.tensor_copy(out=tile[:], in_=raw.bitcast(F32).rearrange("r (a p u) -> r a u p", a=4, u=2))
            for i, slab in enumerate(slabs):
                slab_sorted[slab] = tile[:, 2 * i : 2 * i + 2, :, :]

        def sort_x(m):
            sort_slabs(x_raw[m][:].rearrange("r i k -> r (i k)"), ((m, X_SLAB), (m + 1, X_SLAB)))

        def sort_h(m):
            sort_slabs(h_rows[m][:], ((m, 0), (m, 1)))

        def turn_slab(m, j):
            slab_bank[m, j] = turn_bank()
            for g in range(2):
                for u in range(2):
                    if (m, j) in slab_sorted:
                        pairs = slab_sorted[m, j][:, g, u, :]
                    else:
                        pairs = h_raw[m, j].bitcast(F32)[:, 2 * P * g + u : 2 * P * (g + 1) : 2]
                    nc.tensor.transpose(slab_bank[m, j][:, g, u, :], pairs, ident[:])

        def unload_slab(m, j, copy=nc.scalar.copy):
            slab_grouped[m, j] = grouped_tile()
            copy(
                out=slab_grouped[m, j][:].bitcast(F32).rearrange("p (g r u) -> p g r u", g=2, u=2),
                in_=slab_bank[m, j][:].rearrange("p g u r -> p g r u"),
            )

        def quant_slab(m, j):
            a_code[m, j] = keep.tile([P, 2 * P], U32, name="a_code%d%d" % (m, j), align_bytes=MX_ALIGN)
            a_scale[m, j] = keep.tile([P, 2 * P], U8, name="a_scale%d%d" % (m, j), align_bytes=MX_ALIGN)
            nc.vector.quantize_mx(out=a_code[m, j][:].bitcast(FP8X4), scales=a_scale[m, j][:], in_=slab_grouped[m, j][:])

        w_grouped = {}
        w_code = {}
        w_scale = {}

        def regroup_w(c, g, copy, cols):
            if (c, g) not in w_grouped:
                w_grouped[c, g] = flow.tile([P, N, 4], BF16, name="w_grouped", align_bytes=MX_ALIGN, bufs=3)
            copy(
                out=w_grouped[c, g][:, cols, :].rearrange("p (n i) t -> p n t i", i=4),
                in_=w_raw[c, g][:, :, cols].rearrange("p t (n i) -> p n t i", i=4),
            )

        def regroup_w_scalar(c, g):
            regroup_w(c, g, nc.scalar.copy, slice(0, SCALAR_COLS[c]))

        def regroup_w_vector(c, g):
            regroup_w(c, g, nc.vector.tensor_copy, slice(SCALAR_COLS[c], N))

        def quant_w(c, g):
            w_code[c, g] = keep.tile([P, N], U32, name="w_code%d%d" % (c, g), align_bytes=MX_ALIGN)
            w_scale[c, g] = keep.tile([P, N], U8, name="w_scale%d%d" % (c, g), align_bytes=MX_ALIGN)
            nc.vector.quantize_mx(
                out=w_code[c, g][:].bitcast(FP8X4),
                scales=w_scale[c, g][:],
                in_=w_grouped[c, g][:].rearrange("p n t -> p (n t)"),
            )

        drive = {}

        def drive_bank(m):
            return psum.tile([P, N], F32, name="drive%d" % m)

        def rec_pass(group, g, out, n0, n1):
            c, m = divmod(group, TILES)
            j, rows = g // 2, slice((g % 2) * P, (g % 2 + 1) * P)
            nc.tensor.matmul_mx(
                out=out,
                lhsT=a_code[m, j][:, rows].bitcast(FP8X4),
                lhsT_scale=a_scale[m, j][:, rows],
                rhs=r_code[c, g][:, 2 * n0 : 2 * n1].bitcast(FP4X4),
                rhs_scale=r_scale[c][:, g, n0:n1],
                start=(g == 0),
                stop=False,
            )

        def in_pass(group, g, out, n0, n1):
            c, m = divmod(group, TILES)
            rows = slice(g * P, (g + 1) * P)
            nc.tensor.matmul_mx(
                out=out,
                lhsT=a_code[m, X_SLAB][:, rows].bitcast(FP8X4),
                lhsT_scale=a_scale[m, X_SLAB][:, rows],
                rhs=w_code[c, g][:, n0:n1].bitcast(FP8X4),
                rhs_scale=w_scale[c, g][:, n0:n1],
                start=False,
                stop=(g == IN_PASSES - 1),
            )

        def rec_passes(group, g0=0, g1=REC_PASSES):
            if g0 == 0:
                drive[group] = drive_bank(group % TILES)
            for g in range(g0, g1):
                rec_pass(group, g, drive[group][:], 0, N)

        def in_passes(group):
            for g in range(IN_PASSES):
                in_pass(group, g, drive[group][:], 0, N)

        y = {}
        y_bf = {}
        squashed = {}

        def decay(group):
            c, m = divmod(group, TILES)
            y[group] = keep.tile([P, N], F32, name="y%d" % group)
            old = h_raw[m, c // 2][:, (c % 2) * N : (c % 2 + 1) * N]
            nc.vector.tensor_tensor(out=y[group][:], in0=old, in1=leak_all[:, c * N : (c + 1) * N], op=ALU.mult)

        def squashed_tile():
            return flow.tile([P, N], F32, name="squashed")

        def rounded_tile():
            return flow.tile([P, N], BF16, name="y_bf", bufs=8, align_bytes=MX_ALIGN)

        def squash(group):
            squashed[group] = squashed_tile()
            nc.scalar.activation(out=squashed[group][:], in_=drive[group][:], func=ACT.Tanh)

        def store_y(group):
            c, m = divmod(group, TILES)
            nc.sync.dma_start(out=out_0[m * P : (m + 1) * P, c * N : (c + 1) * N], in_=y[group][:])

        def add_up(group):
            nc.vector.tensor_tensor(out=y[group][:], in0=squashed[group][:], in1=y[group][:], op=ALU.add)
            store_y(group)

        def round_y(group, copy):
            y_bf[group] = rounded_tile()
            copy(
                out=y_bf[group][:].rearrange("r (u p e) -> r u p e", u=2, e=2),
                in_=y[group][:].rearrange("r (p u e) -> r u p e", u=2, e=2),
            )

        y_scale = keep.tile([P, B], U8, name="y_scale", align_bytes=MX_ALIGN)
        y_code = []
        for c in range(CHUNKS):
            y_code.append(keep.tile([P, B], U32, name="y_code%d" % c, align_bytes=MX_ALIGN))
        y_grouped = {}

        def turn_y(c, m0, m1):
            n = m1 - m0
            bank = turn_bank()
            for i in range(n):
                pairs = y_bf[TILES * c + m0 + i][:].bitcast(F32)
                for u in range(2):
                    nc.tensor.transpose(bank[:, i, u, :], pairs[:, u * P : (u + 1) * P], ident[:])
            y_grouped[c, m0] = grouped_tile()
            nc.scalar.copy(
                out=y_grouped[c, m0][:, : n * N].bitcast(F32).rearrange("p (i r u) -> p i r u", i=n, u=2),
                in_=bank[:, :n, :, :].rearrange("p i u r -> p i r u"),
            )

        def quant_y(c, m0, m1):
            rows = slice(m0 * P, m1 * P)
            nc.vector.quantize_mx(
                out=y_code[c][:, rows].bitcast(FP8X4),
                scales=y_scale[4 * c :, rows],
                in_=y_grouped[c, m0][:, : (m1 - m0) * N],
            )
            nc.sync.dma_start(out=y_words[c, :, rows], in_=y_code[c][:, rows].bitcast(I32))


        spread_leak(0)
        turn_slab(0, 0)
        unload_slab(0, 0, nc.vector.tensor_copy)
        quant_slab(0, 0)
        turn_slab(0, 1)
        unload_slab(0, 1)
        spread_leak(1)
        quant_slab(0, 1)
        rec_passes(0, 0, 2)

        turn_slab(1, 0)
        turn_slab(1, 1)
        unload_slab(1, 0)
        regroup_w_scalar(0, 0)
        unload_slab(1, 1)
        for m in range(2):
            decay(m)
            decay(TILES + m)
        sort_h(2)
        regroup_w_vector(0, 0)
        quant_slab(1, 0)
        sort_x(0)
        quant_slab(1, 1)
        rec_passes(0, 2, 4)

        def turn_run(run):
            for m, j in run:
                turn_slab(m, j)
            for m, j in run:
                unload_slab(m, j)

        def quant_run(run):
            for m, j in run:
                quant_slab(m, j)

        run = ((2, 0), (2, 1), (0, X_SLAB))
        turn_run(run)
        regroup_w_scalar(0, 1)
        decay(2)
        quant_w(0, 0)
        regroup_w_vector(0, 1)
        quant_run(run)
        sort_x(2)
        rec_passes(1)

        run = ((1, X_SLAB), (3, 0), (3, 1))
        turn_run(run)
        regroup_w_scalar(1, 0)
        decay(3)
        quant_w(0, 1)
        quant_run(run)
        regroup_w_vector(1, 0)
        rec_passes(2)
        in_passes(0)

        run = ((2, X_SLAB), (3, X_SLAB))
        turn_run(run)
        squash(0)
        regroup_w_scalar(1, 1)
        decay(TILES + 2)
        quant_w(1, 0)
        quant_run(run)
        regroup_w_vector(1, 1)
        in_passes(1)
        rec_passes(3)
        add_up(0)
        squash(1)
        quant_w(1, 1)
        add_up(1)
        round_y(0, nc.scalar.copy)

        first_step = 2
        regroup_at = {3 + 2 * i: (2 + i // IN_PASSES, i % IN_PASSES) for i in range(2 * IN_PASSES)}
        to_decay = list(range(TILES + 3, GROUPS))
        for s in range(first_step, LAST):
            if s >= TILES:
                rec_passes(s)
            in_passes(s)
            if s > first_step:
                squash(s - 1)
                round_y(s - 2, nc.scalar.copy if s - 2 < ROUND_ON_VECTOR_FROM else nc.vector.tensor_copy)
            ready = s // TILES - 1 if s > TILES and s % TILES == TILES - 1 else None
            if ready is not None:
                turn_y(ready, 0, 2)
                turn_y(ready, 2, 4)
            steps_left = LAST - 1 - s
            if to_decay and (s - 1 not in regroup_at or steps_left <= len(to_decay)):
                decay(to_decay[0])
                to_decay = to_decay[1:]
            if s > first_step:
                add_up(s - 1)
            if s - 1 in regroup_at:
                quant_w(*regroup_at[s - 1])
            if s in regroup_at:
                regroup_w_scalar(*regroup_at[s])
                regroup_w_vector(*regroup_at[s])
            if ready is not None:
                quant_y(ready, 0, 2)
                quant_y(ready, 2, 4)

        squash(LAST - 1)
        turn_y(CHUNKS - 2, 0, 2)
        turn_y(CHUNKS - 2, 2, 4)

        half = N // 2
        half_bank = []
        for a, m in enumerate((TILES - 1, 0)):
            half_bank.append(drive_bank(m))
            for quarter in range(2):
                n0 = a * half + quarter * P
                out = half_bank[a][:, quarter * P : (quarter + 1) * P]
                for g in range(REC_PASSES):
                    rec_pass(LAST, g, out, n0, n0 + P)
                for g in range(IN_PASSES):
                    in_pass(LAST, g, out, n0, n0 + P)
        round_y(LAST - 2, nc.vector.tensor_copy)
        add_up(LAST - 1)
        quant_y(CHUNKS - 2, 0, 2)
        round_y(LAST - 1, nc.vector.tensor_copy)
        quant_y(CHUNKS - 2, 2, 4)

        squashed[LAST] = squashed_tile()
        for a in range(2):
            cols = slice(a * half, (a + 1) * half)
            nc.scalar.activation(out=squashed[LAST][:, cols], in_=half_bank[a][:, :half], func=ACT.Tanh)
            nc.vector.tensor_tensor(out=y[LAST][:, cols], in0=squashed[LAST][:, cols], in1=y[LAST][:, cols], op=ALU.add)
        store_y(LAST)
        y_bf[LAST] = rounded_tile()
        for a in range(2):
            nc.vector.tensor_copy(
                out=y_bf[LAST][:].rearrange("r (u p e) -> r u p e", u=2, e=2)[:, :, a * P // 2 : (a + 1) * P // 2, :],
                in_=y[LAST][:, a * half : (a + 1) * half].rearrange("r (p u e) -> r u p e", u=2, e=2),
            )

        turn_y(CHUNKS - 1, 0, 2)
        turn_y(CHUNKS - 1, 2, 3)
        quant_y(CHUNKS - 1, 0, 2)
        quant_y(CHUNKS - 1, 2, 3)
        turn_y(CHUNKS - 1, 3, 4)
        quant_y(CHUNKS - 1, 3, 4)

        for q in range(4):
            queue = nc.sync if q < 2 else nc.scalar
            queue.dma_start(out=y_scales[:, 4 * q : 4 * q + 4, :], in_=y_scale[32 * q : 32 * q + 16, :].bitcast(I32))
